import numpy as np, ml_dtypes
CORES = [66,74,82,90,194,202,210,218]
N = 8
BF = ml_dtypes.bfloat16
L, M, P, RO = 128, 1024, 2, 4
PLANT = [[58, 0, 0], [444, 0, 1], [785, 2, 1], [955, 1, 2], [443, 0, 0]]
LIMS = [[0, 2], [3, 1], [6, 1], [7, 5]]
BRINK = 568
def skew(rng):
    return np.minimum((M * rng.random((N, 8, 16, L)) ** rng.choice(np.array([0.5, 1.0, 2.0]), (N, 8, 16, 1))).astype(np.int64), M - 1)
def parts(rng):
    col = skew(rng); om = np.where(rng.random((N, 8, 16, L)) < rng.choice(np.array([0.4, 0.7, 0.95]), (N, 8, 1, 1)), skew(rng), 0)
    who = np.minimum((16 * rng.random((N, 8, L)) ** rng.choice(np.array([1.5, 2.0, 3.0]), (1, 8, 1))).astype(np.int64), 15)
    order = np.argsort(rng.random((8, 16)), axis=1); mem = order[np.arange(8)[None, :, None], who]
    th = np.minimum(np.maximum(rng.permutation(np.array([1, 2, 3, 4, 6, 8, 9, 11]))[None, :] + rng.integers(-1, 2, (N, 8)), 1), 16)
    return col, om, mem, th
def pack(col, om, mem, th):
    return {"col": np.ascontiguousarray(col.reshape(N, 128, L)).astype(np.int32), "om": np.ascontiguousarray(om.reshape(N, 128, L)).astype(np.int32),
            "mem": np.ascontiguousarray(mem).astype(np.int32), "th": np.ascontiguousarray(th.reshape(N, 8, 1)).astype(np.int32)}
def near(rng, g, col, om, mem, th):
    s = int(rng.integers(0, N)); b = rng.permutation(16)
    col[:, g] = np.maximum(skew(rng)[:, g], 1); om[:, g] = 0; mem[:, g] = b[rng.integers(3, 16, (N, L))]
    for n, k, c in PLANT:
        r, i = (n // L + s) % N, n % L
        mem[r, g, i] = b[k]; om[r, g, b[(k + np.arange(c)) % 16], i] = 1
    for r, v in LIMS: th[(r + s) % N, g] = v
def brink(rng, g, col, om, mem, th):
    b = rng.permutation(16); r, i = BRINK // L, BRINK % L; v = rng.integers(1, M - 1, 2)
    col[:, g] = np.minimum(col[:, g], M - 2); col[:, g, b[2:4]] = 0; col[N - 1, g, b[2:4], L - 1] = v
    om[:, g] = 0; om[r, g, b[2:4], i] = rng.integers(1, v + 1)
    mem[:, g] = b[0]; mem[r, g, i] = b[1]; th[r, g] = 2
def setup_inputs(rng):
    return pack(*parts(rng))
def setup_inputs_lone(rng):
    col, om, mem, th = parts(rng)
    for g in (0, 2, 4, 6): mem[:, g] = rng.integers(0, 16)
    for g in (1, 5): mem[:, g] = ((np.arange(N) + rng.integers(0, 16)) & 15)[:, None]
    a, b = rng.permutation(16)[:2]
    mem[:, 3] = np.where(mem[:, 3] == a, b, mem[:, 3]); mem[N - 1, 3, L - 1] = a
    mem[:, 7] = np.where(mem[:, 7] == b, a, mem[:, 7]); mem[0, 7, 0] = b
    return pack(col, om, mem, th)
def setup_inputs_ties(rng):
    col, om, mem, th = parts(rng)
    v = rng.integers(1, M - 1, (8, 6)); v[:, 0] = 0; v[:, 1] = M - 1; g = np.arange(8)[None, :, None, None]
    col = v[g, rng.integers(0, 6, (N, 8, 16, L))]; om = v[g, rng.integers(0, 6, (N, 8, 16, L))]
    near(rng, int(rng.integers(0, 8)), col, om, mem, th)
    return pack(col, om, mem, th)
def setup_inputs_ends(rng):
    col, om, mem, th = parts(rng); q = rng.permutation(8); th = rng.integers(1, 17, (N, 8))
    col[:, q[:3]] = np.maximum(col[:, q[:3]], 1); om[:, q[:3]] = 1
    om[:, q[1], rng.integers(0, 16)] = 0; om[:, q[2], rng.integers(0, 16)] = 0
    th[:, q[0]] = 16; th[:, q[1]] = 16; th[:, q[2]] = 15; th[rng.integers(0, N), q[1]] = 1
    om[:, q[3]] = 0; th[:, q[3]] = 1; om[:, q[4]] = M - 1; col[:, q[4], ::3] = M - 1; th[:, q[4]] = rng.integers(1, 4, N); th[:, q[5]] = 1
    k, j = rng.permutation(16)[:2]; v = int(rng.integers(1, M - 1))
    c = np.maximum(col[:, q[6]], 1); c = np.where(c == v, v + 1, c); c[:, k] = v; c[v // L, j, v % L] = 0
    col[:, q[6]] = c; om[:, q[6]] = 1; th[:, q[6]] = 16
    brink(rng, int(q[7]), col, om, mem, th)
    return pack(col, om, mem, th)
def setup_inputs_far(rng):
    col, om, mem, th = parts(rng)
    col[:, ::2] = ((np.arange(N) + 1) % N * L)[:, None, None, None] + rng.integers(0, L, (N, 4, 16, L))
    col[:, 1] = rng.integers(0, 16, (N, 16, L)); col[:, 5] = rng.integers(0, 16, (N, 16, L))
    for g in (0, 1, 4, 5): mem[:, g] = rng.permutation(16)[:2][rng.integers(0, 2, (N, L))]
    return pack(col, om, mem, th)
def setup_inputs_spread(rng):
    col, om, mem, th = parts(rng); h = np.log2(M)
    col = np.minimum((np.exp2(h * rng.random((N, 8, 1, L)) ** 0.5) * rng.random((N, 8, 16, L))).astype(np.int64), M - 1)
    om = np.minimum((np.exp2(h * rng.random((N, 8, 16, L))) - 1).astype(np.int64), M - 1)
    th = np.minimum(np.exp2(4.1 * rng.random((N, 8))).astype(np.int64), 16); th[:, rng.integers(0, 8)] = 1
    return pack(col, om, mem, th)
def check_inputs(d):
    bad = []
    for k, lo, hi in (("col", 0, M - 1), ("om", 0, M - 1), ("mem", 0, 15), ("th", 1, 16)):
        if np.min(d[k]) < lo or np.max(d[k]) > hi: bad.append("range of " + k)
    return bad
def reference(col, om, mem, th):
    def joined(a): return np.ascontiguousarray(a.astype(np.int64).reshape(N, 8, 16, L).transpose(1, 2, 0, 3)).reshape(8, 16, M)
    def parted(a): return np.ascontiguousarray(a.reshape(8, 16, N, L).transpose(2, 0, 1, 3)).reshape(N, 128, L)
    vec = np.zeros((8, 16, M * (RO + 1)), np.int64); vec[:, :, :M] = joined(col)
    w = joined(om); R = np.zeros((8, M), np.int64); S = np.zeros((8, M), np.int64)
    one = mem.astype(np.int64).transpose(1, 0, 2).reshape(8, 1, M) == np.arange(16)[None, :, None]
    lim = np.repeat(th.astype(np.int64)[:, :, 0].T, L, axis=1); lane = np.arange(M); i = np.tile(np.arange(L), N); none = 2 ** 20
    hist = []
    for t in range(RO):
        last = vec[:, :, M * t:M * (t + 1)]; e = M * (t + 1) + lane
        par = [(last, w, R)]
        for p in range(P):
            o = (5 * i + (lane - i) + 61 * S + 16 * R + 77 * t + 341 * p) & (M - 1)
            par.append((np.take_along_axis(last, o[:, None, :], 2), np.take_along_axis(w, o[:, None, :], 2), np.take_along_axis(R, o, 1)))
        x = np.where(one, e, np.maximum.reduce([a[0] for a in par]))
        vec[:, :, M * (t + 1):M * (t + 2)] = x
        top = np.maximum.reduce([a[2] for a in par])
        low = np.minimum.reduce([np.where((a[2] == top)[:, None, :] & (a[1] > 0), a[1], none) for a in par])
        c = np.zeros((8, 16, M), np.int64)
        for k in range(16):
            c += np.take_along_axis(vec, x[:, k:k + 1, :], 2) >= low
        S = np.add.reduce((c >= lim[:, None, :]).astype(np.int64), axis=1)
        up = S >= lim; R = top + up
        w = np.where(up[:, None, :], np.where(one, e, 0), np.where(low == none, 0, low))
        hist.append(R)
    yr = np.ascontiguousarray(np.stack(hist).reshape(RO, 8, N, L).transpose(2, 1, 0, 3)).reshape(N, 8, RO * L)
    return {"yx": parted(x).astype(np.float32), "yo": parted(w).astype(np.float32), "yr": yr.astype(np.float32)}

@@ -1,0 +1,482 @@
+from concourse.bass import DstId, RemoteDMATransfer
+from concourse.mybir import AluOpType as A
+from concourse.mybir import ActivationFunctionType as AF
+
+H, F, BF, I, U = "float16", "float32", "bfloat16", "int32", "uint16"
+PSUM = ("pv0", "pv1", "pk0", "pk1", "pe0", "pe1", "px", "py")
+SCRATCH = {
+    "stg": ("dram", [8, 128, 32], I), "lnd": ("dram", [8, 128, 32], I),
+    "stg2": ("dram", [128, 16], I), "lnd2": ("dram", [8, 128, 16], I),
+    "stgx": ("dram", [8, 128, 16], F), "lndx": ("dram", [8, 128, 16], F),
+    "stgw": ("dram", [8, 128, 32], F), "lndw": ("dram", [8, 128, 32], F),
+}
+for _dt, _w, _names in (
+        (I, 128, "i1 i1m j2 li cc oo memr"), (I, 8, "pc r8 th8"), (I, 32, "b0"), (I, 16, "oi oj"),
+        (U, 128, "off"), (U, 16, "o16"),
+        (F, 8, "pf mr mrk thc tu tv"), (F, 128, "nid lane3 xf xs x1 xo k1 k2 ownk mm t2 t3 t4 oe3 wo"),
+        (F, 512, "rh"), (F, 1024, "kt"), (F, 2048, "gb"), (F, 4104, "vt"),
+        (H, 64, "b0f"), (H, 128, "idn am g8 lanec x16 t8 lowt z16 ta tb tq onep onen zb"), (H, 136, "memf"),
+        (H, 1024, "sel"), (H, 2048, "ex"),
+        (BF, 128, "idb idk amb blk sf up"), (BF, 248, "b61"), (BF, 256, "keep sc ft"), (BF, 1024, "selk"),
+        (BF, 2048, "dg f1")):
+    for _n in _names.split():
+        SCRATCH[_n] = ("sbuf", [128, _w], _dt)
+for _n in PSUM:
+    SCRATCH[_n] = ("psum", [128, 512], F)
+SEMAPHORES = ["g", "v", "a", "p", "dstg", "dstg2", "down", "dcc", "doo", "dmem", "dth", "dx", "dxo", "dw", "dwo", "dy",
+              "dyo", "dyr", "dpad", "arr1", "arr2", "arrx", "arrw", "sent"]
+MAGIC = 1.5 * 2.0 ** 36
+HOP = 0.06
+ORDER = {}
+
+
+def needs(ops):
+    writer, readers, deps, follow, lines = {}, {}, [], [], {}
+    for k, (q, fn, rd, wr, sem, busy, lat) in enumerate(ops):
+        line = [w for w in wr if w[0] == "~"]
+        wr = [w for w in wr if w[0] != "~"]
+        d = set()
+        for r in rd:
+            d.update(writer.get(r, []))
+            if r in PSUM:
+                d.update(x for x in readers.get(r, []) if ops[x][0] != q)
+        for w in wr:
+            d.update(writer.get(w, []))
+            d.update(readers.get(w, []))
+        f = set()
+        if q == "p":
+            f = set(x for x in d if ops[x][0] == "p")
+            d -= f
+        for name in line:
+            f.update(lines.get(name, []))
+            lines[name] = [k]
+        for r in rd:
+            readers.setdefault(r, []).append(k)
+        for w in wr:
+            same = sem is not None and w in writer and all(ops[x][4] == sem for x in writer[w]) and not readers.get(w)
+            if same:
+                d -= set(writer[w])
+                writer[w] = writer[w] + [k]
+            else:
+                writer[w] = [k]
+            readers[w] = []
+        d.discard(k)
+        deps.append(d)
+        follow.append(f)
+    return deps, follow
+
+
+def place(ops, deps, follow, rank):
+    n = len(ops)
+    start, slots = [0.0] * n, {}
+    for k in sorted(range(n), key=lambda i: (-rank[i], i)):
+        q, busy = ops[k][0], ops[k][5]
+        s = max([0.0] + [start[x] + ops[x][6] + HOP for x in deps[k]] + [start[x] + ops[x][6] for x in follow[k]])
+        lst = slots.setdefault(q, [])
+        at = len(lst)
+        for i in range(len(lst)):
+            a, b = lst[i]
+            if b <= s:
+                continue
+            if s + busy <= a:
+                at = i
+                break
+            s = b
+        lst.insert(at, (s, s + busy))
+        start[k] = s
+    return sorted(range(n), key=lambda i: (start[i], i))
+
+
+def span(ops, deps, order):
+    total = 0.0
+    for speed, hop in (({}, HOP), ({"a": 1.25}, HOP), ({"p": 1.5}, HOP), ({"v": 1.15, "a": 0.8}, HOP), ({}, 2.5 * HOP)):
+        free, end = {}, {}
+        for k in order:
+            q, f = ops[k][0], speed.get(ops[k][0], 1.0) if ops[k][4] is None else 1.0
+            s = max([free.get(q, 0.0)] + [end[x] + hop for x in deps[k]])
+            free[q] = s + ops[k][5] * f
+            end[k] = s + ops[k][6] * f
+        total += max(end.values())
+    return total
+
+
+def arrange(ops, deps, follow):
+    n = len(ops)
+    if n in ORDER:
+        return ORDER[n]
+
+    def ranks(extra):
+        rank = [0.0] * n
+        for k in range(n - 1, -1, -1):
+            rank[k] += ops[k][6] + extra[k]
+            for x in deps[k]:
+                rank[x] = max(rank[x], rank[k] + HOP)
+            for x in follow[k]:
+                rank[x] = max(rank[x], rank[k])
+        return rank
+
+    seed = [12345]
+
+    def draw():
+        seed[0] = (seed[0] * 6364136223846793005 + 1442695040888963407) % 2 ** 64
+        return (seed[0] >> 11) / 2.0 ** 53
+
+    first = min(k for k in range(n) if "cc" in ops[k][2])
+    extra = [60.0 if k < first and ops[k][4] is None else 0.0 for k in range(n)]
+    order = place(ops, deps, follow, ranks(extra))
+    best = span(ops, deps, order)
+    for it in range(600):
+        other = list(extra)
+        for j in range(6):
+            other[first + int(draw() * (n - first))] = draw() * 1.5 if draw() < 0.6 else 0.0
+        o = place(ops, deps, follow, ranks(other))
+        v = span(ops, deps, o)
+        if v <= best:
+            best, extra, order = v, other, o
+    ORDER[n] = order
+    return order
+
+
+def emit(ops, g, T, arrivals):
+    queues = {"g": g, "v": g.vector, "a": g.scalar, "p": g.tensor, "s": g.sync}
+    deps, follow = needs(ops)
+    order = arrange(ops, deps, follow)
+    pos, count = {}, {}
+    for k in order:
+        src = ops[k][4] if ops[k][4] is not None else ops[k][0]
+        count[src] = count.get(src, 0) + 1
+        pos[k] = (src, count[src])
+    known = {q: {} for q in queues}
+    after, waits, needed = {}, {}, set()
+    for k in order:
+        q = ops[k][0]
+        want = {}
+        for x in deps[k]:
+            src, c = pos[x]
+            if ops[x][1] is not None and ops[x][4] in arrivals:
+                continue
+            if ops[x][4] is not None:
+                c = count[src]
+            if c > want.get(src, (0, 0))[0]:
+                want[src] = (c, x)
+        lst = []
+        if ops[k][1] is not None:
+            for src, (c, x) in sorted(want.items(), key=lambda it: -len(after[it[1][1]])):
+                if known[q].get(src, 0) >= c:
+                    continue
+                lst.append((src, x))
+                needed.add(x)
+                known[q][src] = c
+                for s2, c2 in after[x].items():
+                    if known[q].get(s2, 0) < c2:
+                        known[q][s2] = c2
+        waits[k] = lst
+        after[k] = dict(known[q]) if ops[k][1] is not None else {}
+    val, total = {}, {}
+    for k in order:
+        if ops[k][4] is None and k in needed:
+            total[ops[k][0]] = total.get(ops[k][0], 0) + 1
+            val[k] = total[ops[k][0]]
+    for src in count:
+        if src in arrivals:
+            total[src] = arrivals[src]
+        elif src not in queues:
+            total[src] = 16 * count[src]
+    waited = {}
+    for k in order:
+        q, fn, rd, wr, sem, busy, lat = ops[k]
+        for src, x in waits[k]:
+            c = val[x] if ops[x][4] is None else total[src]
+            queues[q].wait_ge(T.sem[src], c)
+            waited[src] = max(waited.get(src, 0), c)
+        if fn is None:
+            continue
+        ins = fn()
+        if sem is None:
+            if k in needed:
+                ins.then_inc(T.sem[q], 1)
+        elif sem not in arrivals:
+            ins.then_inc(T.sem[sem], 16)
+    for src in sorted(total):
+        if waited.get(src, 0) < total[src]:
+            g.wait_ge(T.sem[src], total[src])
+
+
+def rank_program(g, core, T, topo):
+    me = T.rank_of(core)
+    if me is None:
+        return
+    cores = list(T.cores)
+    others = [r for r in range(8) if r != me]
+    V, S, P = g.vector, g.scalar, g.tensor
+    ops = []
+
+    def op(q, fn, rd, wr, sem=None, busy=0.16, lat=None):
+        ops.append((q, fn, rd.split(), wr.split(), sem, busy, busy if lat is None else lat))
+
+    def vt_(n):
+        return 0.03 + 0.001 * max(64, n)
+
+    def ts(out, in0, s1, s2, op0, op1, rd, wr, n=128):
+        if s2 is None:
+            op("v", lambda: V.tensor_scalar(out, in0, s1, None, op0), rd, wr, busy=vt_(n))
+        else:
+            op("v", lambda: V.tensor_scalar(out, in0, s1, s2, op0, op1), rd, wr, busy=vt_(n))
+
+    def t1(out, in0, s1, op0, rd, wr, n=128):
+        ts(out, in0, s1, None, op0, None, rd, wr, n)
+
+    def tt(out, in0, in1, o, rd, wr, n=128):
+        op("v", lambda: V.tensor_tensor(out, in0, in1, o), rd, wr, busy=vt_(n))
+
+    def cp(out, in_, rd, wr, n=128):
+        op("v", lambda: V.tensor_copy(out, in_), rd, wr, busy=vt_(n))
+
+    def fill(out, c, rd, wr, n=64):
+        op("v", lambda: V.memset(out, c), rd, wr, busy=vt_(n))
+
+    def act(out, in_, rd, wr, scale=None, busy=0.17):
+        if scale is None:
+            op("a", lambda: S.activation(out, in_, AF.Copy), rd, wr, busy=busy)
+        else:
+            op("a", lambda: S.activation(out, in_, AF.Copy, scale=scale), rd, wr, busy=busy)
+
+    def mmul(out, lhs, rhs, start, stop, rd, wr, n=128):
+        op("p", lambda: P.matmul(out, lhs, rhs, start, stop), rd, wr, busy=0.0005 * max(64, n))
+
+    def dma(q, out, in_, rd, wr, sem):
+        eng = g.sync if q == "s" else g.scalar
+        op(q, lambda: eng.dma_start(out, in_), rd, wr, sem, 0.08, 2.3)
+
+    def iota(out, pattern, base, cm, name, n):
+        op("g", lambda: g.iota(out, pattern, base, cm), "", name, busy=0.13 + 0.002 * n)
+
+    def names(stem, n):
+        return " " + " ".join(stem + str(k) for k in range(n))
+
+    def exchange(src, dst, rd, arr, name):
+        trs = []
+        used = 0
+        for r in others:
+            rid, pid = topo.addr(cores[r], core)
+            e = [x for x in topo.engines(core, cores[r]) if not used >> x & 1][0]
+            used |= 1 << e
+            trs.append(RemoteDMATransfer(dst_ids=[DstId(rid=rid, pnc=pid)], dma_engine_mask=1 << e,
+                                         remote_sem=T.sem[arr], src=src(r), dst=dst))
+        op("g", lambda: g.remote_dma_fused(trs, local_sem=T.sem.sent), rd, "call" + arr, "sent", 0.5, 3.5)
+        op("n", None, "call" + arr, name, arr, 0.0, 0.001)
+
+    arrivals = {"arr1": 7, "arr2": 7, "arrx": 7, "arrw": 7, "sent": 28}
+    mine = slice(16 * me, 16 * me + 16)
+
+    dma("s", T.stg[:, 0:64, :], T.col[:], "", "stg", "dstg")
+    dma("a", T.stg[:, 64:128, :], T.om[:], "", "stg", "dstg")
+    dma("s", T.stg2[0:64, :], T.mem[:], "", "stg2", "dstg2")
+    dma("a", T.stg2[64, 0:8], T.th[:], "", "stg2", "dstg2")
+    dma("s", T.stg2[65:128, :], T.mem[:, 0:126], "", "stg2", "dstg2")
+    dma("a", T.stg2[64, 8:16], T.th[:], "", "stg2", "dstg2")
+    dma("s", T.lnd[me, 0:64, :], T.col[mine, :], "", "own", "down")
+    dma("a", T.lnd[me, 64:128, :], T.om[mine, :], "", "own", "down")
+    dma("s", T.lnd2[me, 8 * me:8 * me + 8, :], T.mem[me, :], "", "own", "down")
+    dma("a", T.lnd2[me, 64, 0:8], T.th[:], "", "own", "down")
+    iota(T.pc[:, 0:1], [[0, 1]], 0, 1, "pc0", 1)
+    iota(T.i1[:], [[-1, 128]], 128, 1, "i1", 128)
+    iota(T.j2[:], [[1, 8], [0, 16]], 0, 0, "j2", 128)
+    iota(T.r8[:], [[1, 8]], 0, 0, "r8", 8)
+    iota(T.b0[:], [[77, 4], [80, 8]], 0, 5, "b0", 32)
+    iota(T.li[:], [[1, 128]], 0, 0, "li", 128)
+    exchange(lambda r: T.stg[r], T.lnd[me], "stg", "arr1", "lnd")
+    exchange(lambda r: T.stg2[:], T.lnd2[me], "stg2", "arr2", "lnd2")
+    dma("s", T.cc[:], T.lnd[:, 0:64, :], "lnd own", "cc", "dcc")
+    dma("a", T.oo[:], T.lnd[:, 64:128, :], "lnd own", "oo", "doo")
+    dma("s", T.memr[0:8, :], T.lnd2[:, 8 * me:8 * me + 8, :], "lnd2 own", "memr", "dmem")
+    dma("s", T.th8[0:8, :], T.lnd2[:, 64, 0:8], "lnd2 own", "th8", "dth")
+
+    fill(T.b61[:], 0.0, "", "b61z", 124)
+    fill(T.keep[:], 1.0, "", "keep0", 128)
+    fill(T.vt[:, 1024:4104:1024], -3000.0, "", "vt0")
+    fill(T.keep[:, 0:256:16], 0.0, "keep0", "keep")
+    t1(T.b0f[:], T.i1[:, 0:64], 0.0, A.mult, "i1", "b0f", 64)
+    t1(T.pc[:, 1:2], T.pc[:, 0:1], 4, A.arith_shift_right, "pc0", "pc1", 1)
+    t1(T.pc[:, 2:3], T.pc[:, 0:1], 15, A.bitwise_and, "pc0", "pc2", 1)
+    t1(T.i1m[:], T.i1[:], 15, A.bitwise_and, "i1", "i1m")
+    t1(T.idn[:], T.i1[:], 128.0, A.is_equal, "i1", "idn")
+    cp(T.pf[:, 0:3], T.pc[:, 0:3], "pc0 pc1 pc2", "pf", 3)
+    t1(T.am[:], T.i1m[:], 0.0, A.is_equal, "i1m", "am")
+    t1(T.mr[:], T.r8[:], T.pf[:, 1:2], A.is_equal, "r8 pf", "mr", 8)
+    t1(T.pf[:, 3:4], T.pf[:, 1:2], 48.0, A.mult, "pf", "pf3", 1)
+    t1(T.pf[:, 4:5], T.pf[:, 1:2], 128.0, A.mult, "pf", "pf4", 1)
+    t1(T.g8[0:8, :], T.j2[0:8, :], T.pf[0:8, 0:1], A.is_equal, "j2 pf", "g8")
+    for r in range(8):
+        t1(T.sel[:, 128 * r:128 * r + 128], T.am[:], T.mr[:, r:r + 1], A.mult, "am mr", "sel%d" % r, 64)
+    for t in range(4):
+        t1(T.b0f[:, 16 * t + 8:16 * t + 16], T.b0[:, 8 * t:8 * t + 8], T.pf[:, 3:4], A.add, "b0 pf3 b0f", "b0f%d" % t, 8)
+    cp(T.oi[:, 0:8], T.b0f[:, 8:16], "b0f0", "oi0", 8)
+    t1(T.oi[:, 8:16], T.b0f[:, 8:16], 341.0, A.add, "b0f0", "oi1", 8)
+    t1(T.oj[:], T.oi[:], 1023, A.bitwise_and, "oi0 oi1", "oj", 16)
+    cp(T.o16[:], T.oj[:], "oj", "o16", 16)
+    ts(T.lanec[:], T.li[:], T.pf[:, 4:5], 1024.0 - 2048.0, A.add, A.add, "li pf4", "lanec")
+    ts(T.lane3[:], T.li[:], T.pf[:, 4:5], 4096.0, A.add, A.add, "li pf4", "lane3")
+    for k in range(16):
+        cp(T.ex[:, k:2048:16], T.idn[:], "idn", "ex%d" % k, 64)
+    t1(T.blk[:], T.j2[:], T.pf[:, 1:2], A.is_equal, "j2 pf", "blk")
+    t1(T.b61[:, 120:128], T.mr[:], 61.0, A.mult, "mr b61z", "b61", 8)
+    t1(T.nid[:], T.idn[:], -1.0, A.mult, "idn", "nid")
+    t1(T.idk[:], T.idn[:], 8192.0, A.mult, "idn", "idk", 64)
+    cp(T.idb[:], T.idn[:], "idn", "idb", 64)
+    t1(T.amb[:], T.i1m[:], 0.0, A.is_equal, "i1m", "amb")
+    t1(T.mrk[:], T.mr[:], 8192.0, A.mult, "mr", "mrk", 8)
+    for r in range(8):
+        act(T.selk[:, 128 * r:128 * r + 128], T.amb[:], "amb mrk", "selk%d" % r, T.mrk[:, r:r + 1])
+    for a in range(16):
+        act(T.dg[:, a:2048:16], T.b61[:, 120 - 8 * a:248 - 8 * a], "b61", "dg%d" % a)
+    sels, selks, exs, dgs = names("sel", 8), names("selk", 8), names("ex", 16), names("dg", 16)
+
+    def repeat(b, h, name, mats, mname, start, stop):
+        for r in range(4 * h, 4 * h + 4):
+            c = 128 * (r % 4)
+            mmul(T[b][:, c:c + 128], mats[:, 128 * r:128 * r + 128], T[name][:],
+                 start is True or (start == "first" and r % 4 == 0),
+                 stop is True or (stop == "last" and r % 4 == 3), name + mname, b + " ~" + b[:2])
+
+    def table(dst, c0, b, name):
+        act(dst[:, c0:c0 + 512], T[b][:], b, name, busy=0.56)
+
+    t1(T.x16[:], T.cc[:], -2048.0, A.add, "cc", "x16")
+    repeat("pv0", 0, "x16", T.sel, sels, True, True)
+    repeat("pv1", 1, "x16", T.sel, sels, True, True)
+    table(T.vt, 0, "pv0", "vt0_0")
+    table(T.vt, 512, "pv1", "vt0_1")
+    ts(T.ta[:], T.oo[:], 0.0, -6048.0, A.is_equal, A.mult, "oo", "ta")
+    ts(T.tb[:], T.oo[:], -1.0, 2048.0, A.mult, A.add, "oo", "tb")
+    cp(T.memf[0:8, 0:128], T.memr[0:8, :], "memr", "memf0")
+    tt(T.z16[:], T.ta[:], T.tb[:], A.add, "ta tb", "z16", 256)
+    mmul(T.px[:, 0:128], T.g8[0:8, :], T.memf[0:8, 0:128], True, True, "g8 memf0", "px")
+    repeat("pk0", 0, "z16", T.sel, sels, True, True)
+    repeat("pk1", 1, "z16", T.sel, sels, True, True)
+    table(T.kt, 0, "pk0", "kt0")
+    table(T.kt, 512, "pk1", "kt1")
+    ts(T.tq[:], T.px[:, 0:128], T.pf[:, 2:3], -8192.0, A.not_equal, A.mult, "px pf", "tq")
+    mmul(T.py[:, 0:128], T.idn[:], T.lanec[:], True, False, "idn lanec", "py")
+    mmul(T.py[:, 0:128], T.idn[:], T.tq[:], False, True, "idn tq", "py")
+    cp(T.memf[0:8, 128:136], T.th8[0:8, :], "th8", "memf1", 8)
+    tt(T.xs[:], T.x16[:], T.py[:, 0:128], A.max, "py x16", "xs")
+    mmul(T.px[:, 128:136], T.g8[0:8, :], T.memf[0:8, 128:136], True, True, "g8 memf1", "px", 64)
+    ts(T.onep[:], T.tq[:], 0.125, 1024.0, A.mult, A.add, "tq", "onep", 64)
+    mmul(T.px[:, 256:384], T.idn[:], T.onep[:], True, True, "idn onep", "px")
+    cp(T.thc[:, 0:1], T.px[:, 128 + me:129 + me], "px", "thc0", 1)
+    t1(T.onen[:], T.onep[:], -1.0, A.mult, "onep", "onen", 64)
+    tt(T.t3[:], T.tq[:], T.lanec[:], A.subtract, "tq lanec", "t3", 256)
+    t1(T.zb[:], T.t3[:], -4000.0, A.max, "t3", "zb")
+    t1(T.thc[:, 1:2], T.thc[:, 0:1], 61.0, A.mult, "thc0", "thc1", 1)
+    t1(T.t4[:], T.onep[:], 8.0, A.mult, "onep", "t4")
+    tt(T.oe3[:], T.t4[:], T.lane3[:], A.min, "t4 lane3", "oe3", 256)
+
+    ends = [0, 16, 48, 80, 112, 128]
+    sums = {1: (0, 48), 3: (48, 112)}
+    vts = " vt0"
+    for t in range(4):
+        last = t == 3
+        B = 1024 * (t + 1)
+        new = " vt%d_0 vt%d_1" % (t, t)
+        vts += new
+        xn = "xf" if last else "x16"
+        x = T[xn]
+        win = T.vt[:, B - 1024:B]
+        low = T.py[:, 384:512]
+        tt(T.x1[:], win.indirect(T.o16[:, 0:8]), T.xs[:], A.max, "o16 xs" + new, "x1", 220)
+        tt(x[:], win.indirect(T.o16[:, 8:16]), T.x1[:], A.max, "o16 x1" + new, xn, 220)
+        ts(T.off[:], x[:], B - 2048.0, 2048.0, A.min, A.add, xn, "off", 128 if last else 64)
+        for c in range(5):
+            lo, hi = ends[c], ends[c + 1]
+            act(T.gb[:, 16 * lo:16 * hi], T.vt[:, 0:B + 1].indirect(T.off[:, lo:hi]), "off" + vts, "gb%d ~gb" % c,
+                busy=0.06 + 0.025 * (hi - lo))
+        own = "z16" if t == 0 else "ownk"
+        tt(T.k1[:], T.kt[:].indirect(T.o16[:, 0:8]), T[own][:], A.max, "kt0 kt1 o16 " + own, "k1", 220)
+        tt(T.k2[:], T.kt[:].indirect(T.o16[:, 8:16]), T.k1[:], A.max, "kt0 kt1 o16 k1", "k2", 220)
+        ts(T.t8[:], T.k2[:], MAGIC, -MAGIC, A.add, A.add, "k2", "t8")
+        mmul(T.py[:, 0:128], T.k2[:], T.nid[:], True, False, "k2 nid", "py", 512)
+        mmul(T.py[:, 0:128], T.t8[:], T.idn[:], False, True, "t8 idn", "py")
+        cp(T.lowt[:], T.py[:, 0:128], "py", "lowt")
+        mmul(low, T.lowt[:], T.idn[:], True, True, "lowt idn", "py")
+        if last:
+            t1(T.xo[:], T.xf[:], 2048.0, A.add, "xf", "xo")
+            dma("s", T.stgw[:, 80:128, :], T.lane3[:, 0:96], "lane3 xf", "pad", "dpad")
+            dma("s", T.stgx[:], T.xo[:], "xo", "stgx", "dx")
+            dma("s", T.lndx[me], T.xo[mine, :], "xo", "ownx", "dxo")
+            exchange(lambda r: T.stgx[r], T.lndx[me], "stgx", "arrx", "lndx")
+            dma("s", T.yx[:], T.lndx[:], "lndx ownx", "", "dy")
+            t1(T.t2[:], low, 3500.0, A.is_lt, "py", "t2")
+            t1(T.pv0[:, 0:128], low, 2048.0, A.add, "py", "pv0")
+            tt(T.pv1[:, 0:128], T.t2[:], T.pv0[:, 0:128], A.mult, "t2 pv0", "pv1")
+            tt(T.py[:, 128:256], T.oe3[:], T.pv1[:, 0:128], A.subtract, "oe3 pv1", "py")
+        else:
+            repeat("pv0", 0, "x16", T.sel, sels, True, True)
+            repeat("pv1", 1, "x16", T.sel, sels, True, True)
+            t1(T.ft[:, 128:256], T.t8[:], 21.0 / 8192.0, A.mult, "t8", "ft1", 64)
+            tt(T.xs[:], T.x16[:], T.px[:, 256:384], A.add, "x16 px", "xs")
+            repeat("pk0", 0, "t8", T.sel, sels, "first", False)
+            repeat("pk1", 1, "t8", T.sel, sels, "first", False)
+            for n, name in enumerate(["zb"] + ["onen"] * t):
+                mmul(T.py[:, 128:256], T.idn[:], T[name][:], n == 0, False, "idn " + name, "py")
+            mmul(T.py[:, 128:256], T.lowt[:], T.idn[:], False, True, "lowt idn", "py")
+        tt(T.sf[:], x[:], low, A.is_ge, xn + " py", "sf")
+        for c in range(5):
+            lo, hi = ends[c], ends[c + 1]
+            b = "pe%d" % (c % 2)
+            w = 16 * (hi - lo)
+            mmul(T[b][:, 0:w], T.lowt[:], T.ex[:, 16 * lo:16 * hi], True, True, "lowt" + exs, b + " ~ex", w)
+            tt(T.f1[:, 16 * lo:16 * hi], T.gb[:, 16 * lo:16 * hi], T[b][:, 0:w], A.is_ge, "gb%d %s" % (c, b), "f1_%d ~f1" % c, w)
+            if c in sums:
+                l0, l1 = sums[c]
+                if c == 3:
+                    mmul(T.px[:, 0:l0], T.idb[:], T.sf[:, 0:l0], False, False, "idb sf", "px", l0)
+                    mmul(T.px[:, l0:128], T.idb[:], T.sf[:, l0:128], False, False, "idb sf", "px", 128 - l0)
+                for k in range(16):
+                    mmul(T.px[:, l0:l1], T.idb[:], T.f1[:, 16 * l0 + k:16 * l1:16], c == 1 and k == 0, False,
+                         "idb f1_%d f1_%d" % (c - 1, c), "px", 64)
+        op("v", lambda: V.tensor_tensor_scan(T.sc[:], T.keep[:], T.f1[:, 1792:2048], 0.0, A.mult, A.add), "keep f1_4", "sc")
+        mmul(T.px[:, 112:128], T.idb[:], T.sc[:, 15:256:16], False, True, "idb sc", "px", 64)
+        if t > 0:
+            act(T.rh[:, 128 * t - 128:128 * t], T.py[:, 256:384], "py", "rh%d" % (t - 1), 1.0 / 8192.0)
+        if not last:
+            table(T.vt, B, "pv0", "vt%d_0" % (t + 1) + vts)
+            table(T.vt, B + 512, "pv1", "vt%d_1" % (t + 1))
+        t1(T.ft[:, 0:128], T.px[:, 0:128], T.thc[:, 0:1], A.is_ge, "px thc0", "ft0")
+        mmul(T.py[:, 0:128], T.blk[:], T.ft[:, 0:128], True, True, "blk ft0", "py")
+        if not last:
+            mmul(T.px[:, 0:16], T.idn[:], T.b0f[:, 16 * (t + 1):16 * (t + 2)], True, False, "idn b0f%d" % (t + 1), "px", 64)
+            for a in range(16):
+                mmul(T.px[:, 0:16], T.dg[:, 128 * a:128 * a + 128], T.ft[:, a:256:16], False, a == 15, "ft0 ft1" + dgs, "px", 64)
+        t1(T.up[:], T.py[:, 0:128], T.thc[:, 0:1], A.is_ge, "py thc0", "up")
+        tt(T.mm[:], T.py[:, 128:256], T.up[:], A.mult, "py up", "mm")
+        if last:
+            mmul(T.pe1[:, 0:128], T.idn[:], T.t8[:], True, False, "idn t8", "pe1")
+            mmul(T.pe1[:, 0:128], T.idk[:], T.up[:], False, True, "idk up", "pe1")
+            act(T.rh[:, 384:512], T.pe1[:, 0:128], "pe1", "rh3", 1.0 / 8192.0)
+            tt(T.wo[:], T.mm[:], T.pv1[:, 0:128], A.add, "mm pv1", "wo")
+            break
+        tt(T.z16[:], T.mm[:], low, A.subtract, "mm py", "z16")
+        for h, b in enumerate(("pk0", "pk1")):
+            repeat(b, h, "up", T.selk, selks, False, False)
+            repeat(b, h, "z16", T.sel, sels, False, "last")
+            table(T.kt, 512 * h, b, "kt%d" % h)
+        mmul(T.py[:, 256:384], T.idn[:], T.t8[:], True, False, "idn t8", "py")
+        mmul(T.py[:, 256:384], T.idk[:], T.up[:], False, True, "idk up", "py")
+        tt(T.ownk[:], T.z16[:], T.py[:, 256:384], A.add, "z16 py", "ownk")
+        ts(T.tu[:], T.px[:, 0:8], T.thc[:, 1:2], 16.0, A.is_ge, A.mult, "px thc1", "tu", 8)
+        tt(T.tv[:], T.px[:, 0:8], T.tu[:], A.add, "px tu", "tv", 8)
+        tt(T.oi[:, 0:8], T.px[:, 8:16], T.tv[:], A.add, "px tv", "oi0", 8)
+        t1(T.oi[:, 8:16], T.oi[:, 0:8], 341.0, A.add, "oi0", "oi1", 8)
+        t1(T.oj[:], T.oi[:], 1023, A.bitwise_and, "oi0 oi1", "oj", 16)
+        cp(T.o16[:], T.oj[:], "oj", "o16", 16)
+
+    rs = names("rh", 4)
+    dma("a", T.stgw[:, 64:80, :], T.rh[0:128:16, :], rs, "stgw", "dw")
+    dma("s", T.stgw[:, 0:64, :], T.wo[:], "wo", "stgw", "dw")
+    dma("a", T.lndw[me, 64:80, :], T.rh[16 * me:16 * me + 1, :], rs, "ownw", "dwo")
+    dma("s", T.lndw[me, 0:64, :], T.wo[mine, :], "wo", "ownw", "dwo")
+    exchange(lambda r: T.stgw[r], T.lndw[me], "stgw pad", "arrw", "lndw")
+    dma("s", T.yo[:], T.lndw[:, 0:64, :], "lndw ownw", "", "dyo")
+    dma("a", T.yr[:], T.lndw[:, 64:80, :], "lndw ownw", "", "dyr")
+    emit(ops, g, T, arrivals)

@@ -6,12 +6,14 @@ H, F, BF, I, U = "float16", "float32", "bfloat16", "int32", "uint16"
 PSUM = ("pv0", "pv1", "pk0", "pk1", "pe0", "pe1", "px", "py")
 SCRATCH = {
     "stg": ("dram", [8, 128, 32], I), "lnd": ("dram", [8, 128, 32], I),
-    "stg2": ("dram", [128, 16], I), "lnd2": ("dram", [8, 128, 16], I),
+    "stg2": ("dram", [8, 128, 2], I), "lnd2": ("dram", [8, 128, 2], I),
+    "stg3": ("dram", [128, 2], I), "lnd3": ("dram", [8, 128, 2], I),
     "stgx": ("dram", [8, 128, 16], F), "lndx": ("dram", [8, 128, 16], F),
-    "stgw": ("dram", [8, 128, 32], F), "lndw": ("dram", [8, 128, 32], F),
+    "stgw": ("dram", [8, 128, 16], F), "lndw": ("dram", [8, 128, 16], F),
+    "stgr": ("dram", [8, 128, 4], F), "lndr": ("dram", [8, 128, 4], F),
 }
 for _dt, _w, _names in (
-        (I, 128, "i1 i1m j2 li cc oo memr"), (I, 8, "pc r8 th8"), (I, 32, "b0"), (I, 16, "oi oj"),
+        (I, 128, "i1 i1m j2 li cc oo memr"), (I, 8, "pc th8"), (I, 32, "b0"), (I, 16, "oi oj"),
         (U, 128, "off"), (U, 16, "o16"),
         (F, 8, "pf mr mrk thc tu tv"), (F, 128, "nid lane3 xf xs x1 xo k1 k2 ownk mm t2 t3 t4 oe3 wo"),
         (F, 512, "rh"), (F, 1024, "kt"), (F, 2048, "gb"), (F, 4104, "vt"),
@@ -23,10 +25,11 @@ for _dt, _w, _names in (
         SCRATCH[_n] = ("sbuf", [128, _w], _dt)
 for _n in PSUM:
     SCRATCH[_n] = ("psum", [128, 512], F)
-SEMAPHORES = ["g", "v", "a", "p", "dstg", "dstg2", "down", "dcc", "doo", "dmem", "dth", "dx", "dxo", "dw", "dwo", "dy",
-              "dyo", "dyr", "dpad", "arr1", "arr2", "arrx", "arrw", "sent"]
+SEMAPHORES = ["g", "v", "a", "p", "dstg", "dstg2", "down", "down2", "dcc", "doo", "dmem", "dth", "dx", "dxo", "dw", "dwo",
+              "dr", "dro", "dy", "dyo", "dyr", "arr1", "arr2", "arr3", "arrx", "arrw", "arrr", "sent"]
 MAGIC = 1.5 * 2.0 ** 36
 HOP = 0.06
+SPEEDS = (({}, HOP), ({"a": 1.25}, HOP), ({"p": 1.4}, HOP), ({"v": 1.15, "a": 0.8}, HOP), ({}, 2.5 * HOP))
 ORDER = {}
 
 
@@ -71,7 +74,7 @@ def place(ops, deps, follow, rank):
     start, slots = [0.0] * n, {}
     for k in sorted(range(n), key=lambda i: (-rank[i], i)):
         q, busy = ops[k][0], ops[k][5]
-        s = max([0.0] + [start[x] + ops[x][6] + HOP for x in deps[k]] + [start[x] + ops[x][6] for x in follow[k]])
+        s = max([0.0] + [start[x] + ops[x][6] + HOP for x in deps[k]] + [start[x] + ops[x][5] for x in follow[k]])
         lst = slots.setdefault(q, [])
         at = len(lst)
         for i in range(len(lst)):
@@ -87,34 +90,28 @@ def place(ops, deps, follow, rank):
     return sorted(range(n), key=lambda i: (start[i], i))
 
 
-def span(ops, deps, order):
-    total = 0.0
-    for speed, hop in (({}, HOP), ({"a": 1.25}, HOP), ({"p": 1.5}, HOP), ({"v": 1.15, "a": 0.8}, HOP), ({}, 2.5 * HOP)):
-        free, end = {}, {}
-        for k in order:
-            q, f = ops[k][0], speed.get(ops[k][0], 1.0) if ops[k][4] is None else 1.0
-            s = max([free.get(q, 0.0)] + [end[x] + hop for x in deps[k]])
-            free[q] = s + ops[k][5] * f
-            end[k] = s + ops[k][6] * f
-        total += max(end.values())
-    return total
+def span(ops, deps, order, which):
+    speed, hop = SPEEDS[which]
+    free, last, end, held = {}, {}, {}, {}
+    for k in order:
+        q = ops[k][0]
+        f = speed.get(q, 1.0) if ops[k][4] is None else 1.0
+        s, by = free.get(q, 0.0), last.get(q)
+        for x in deps[k]:
+            if end[x] + hop > s:
+                s, by = end[x] + hop, x
+        free[q] = s + ops[k][5] * f
+        last[q] = k
+        end[k] = s + ops[k][6] * f
+        held[k] = by
+    k = max(end, key=end.get)
+    return end[k], held, k
 
 
 def arrange(ops, deps, follow):
     n = len(ops)
     if n in ORDER:
         return ORDER[n]
-
-    def ranks(extra):
-        rank = [0.0] * n
-        for k in range(n - 1, -1, -1):
-            rank[k] += ops[k][6] + extra[k]
-            for x in deps[k]:
-                rank[x] = max(rank[x], rank[k] + HOP)
-            for x in follow[k]:
-                rank[x] = max(rank[x], rank[k])
-        return rank
-
     seed = [12345]
 
     def draw():
@@ -122,19 +119,46 @@ def arrange(ops, deps, follow):
         return (seed[0] >> 11) / 2.0 ** 53
 
     first = min(k for k in range(n) if "cc" in ops[k][2])
-    extra = [60.0 if k < first and ops[k][4] is None else 0.0 for k in range(n)]
-    order = place(ops, deps, follow, ranks(extra))
-    best = span(ops, deps, order)
-    for it in range(600):
-        other = list(extra)
-        for j in range(6):
-            other[first + int(draw() * (n - first))] = draw() * 1.5 if draw() < 0.6 else 0.0
-        o = place(ops, deps, follow, ranks(other))
-        v = span(ops, deps, o)
-        if v <= best:
-            best, extra, order = v, other, o
-    ORDER[n] = order
-    return order
+    rank = [0.0] * n
+    for k in range(n - 1, -1, -1):
+        rank[k] += ops[k][6] + (60.0 if k < first and ops[k][4] is None else 0.0)
+        for x in deps[k]:
+            rank[x] = max(rank[x], rank[k] + HOP)
+        for x in follow[k]:
+            rank[x] = max(rank[x], rank[k])
+    order = place(ops, deps, follow, rank)
+    before = [deps[k] | follow[k] for k in range(n)]
+    runs = [span(ops, deps, order, w) for w in range(len(SPEEDS))]
+    cost = sum(r[0] for r in runs)
+    best, kept, steps = cost, order, 9000
+    for it in range(steps):
+        _, held, k = runs[int(draw() * len(runs))]
+        pairs = []
+        while held[k] is not None:
+            if ops[held[k]][0] == ops[k][0] and held[k] not in before[k]:
+                pairs.append((held[k], k))
+            k = held[k]
+        if not pairs:
+            break
+        j, k = pairs[int(draw() * len(pairs))]
+        a, b = order.index(j), order.index(k)
+        behind, rest = {j}, []
+        for x in order[a + 1:b + 1]:
+            if before[x] & behind:
+                behind.add(x)
+            else:
+                rest.append(x)
+        if k in behind:
+            continue
+        o = order[:a] + rest + [x for x in order[a:b + 1] if x in behind] + order[b + 1:]
+        rs = [span(ops, deps, o, w) for w in range(len(SPEEDS))]
+        v = sum(r[0] for r in rs)
+        if v <= cost + 0.6 * draw() * (1.0 - it / steps):
+            cost, order, runs = v, o, rs
+            if v < best:
+                best, kept = v, o
+    ORDER[n] = kept
+    return kept
 
 
 def emit(ops, g, T, arrivals):
@@ -244,6 +268,12 @@ def rank_program(g, core, T, topo):
     def mmul(out, lhs, rhs, start, stop, rd, wr, n=128):
         op("p", lambda: P.matmul(out, lhs, rhs, start, stop), rd, wr, busy=0.0005 * max(64, n))
 
+    def join(n):
+        part = ops[-n:]
+        del ops[-n:]
+        busy = sum(x[5] for x in part)
+        ops.append(("p", lambda: [x[1]() for x in part][-1], sum((x[2] for x in part), []), part[0][3], None, busy, busy))
+
     def dma(q, out, in_, rd, wr, sem):
         eng = g.sync if q == "s" else g.scalar
         op(q, lambda: eng.dma_start(out, in_), rd, wr, sem, 0.08, 2.3)
@@ -254,48 +284,54 @@ def rank_program(g, core, T, topo):
     def names(stem, n):
         return " " + " ".join(stem + str(k) for k in range(n))
 
-    def exchange(src, dst, rd, arr, name):
-        trs = []
-        used = 0
+    def exchange(src, dst, rd, arr, name, common=None):
+        trs, ids, used, free = [], [], 0, -1
         for r in others:
             rid, pid = topo.addr(cores[r], core)
+            ids.append(DstId(rid=rid, pnc=pid))
             e = [x for x in topo.engines(core, cores[r]) if not used >> x & 1][0]
             used |= 1 << e
-            trs.append(RemoteDMATransfer(dst_ids=[DstId(rid=rid, pnc=pid)], dma_engine_mask=1 << e,
-                                         remote_sem=T.sem[arr], src=src(r), dst=dst))
-        op("g", lambda: g.remote_dma_fused(trs, local_sem=T.sem.sent), rd, "call" + arr, "sent", 0.5, 3.5)
+            free &= topo.mask(core, cores[r])
+            trs.append(RemoteDMATransfer(dst_ids=[ids[-1]], dma_engine_mask=1 << e, remote_sem=T.sem[arr], src=src(r), dst=dst))
+        if common is not None:
+            free &= ~used
+            trs.append(RemoteDMATransfer(dst_ids=ids, dma_engine_mask=free & -free, remote_sem=T.sem[common[2]],
+                                         src=common[0], dsts=[common[1]] * len(ids)))
+        op("g", lambda: g.remote_dma_fused(trs, local_sem=T.sem.sent), rd, "~calls call" + arr, "sent", 0.5, 3.5)
         op("n", None, "call" + arr, name, arr, 0.0, 0.001)
+        if common is not None:
+            op("n", None, "call" + arr, common[3], common[2], 0.0, 0.001)
 
-    arrivals = {"arr1": 7, "arr2": 7, "arrx": 7, "arrw": 7, "sent": 28}
+    arrivals = {"arr1": 7, "arr2": 7, "arr3": 7, "arrx": 7, "arrw": 7, "arrr": 7, "sent": 36}
     mine = slice(16 * me, 16 * me + 16)
 
-    dma("s", T.stg[:, 0:64, :], T.col[:], "", "stg", "dstg")
-    dma("a", T.stg[:, 64:128, :], T.om[:], "", "stg", "dstg")
-    dma("s", T.stg2[0:64, :], T.mem[:], "", "stg2", "dstg2")
-    dma("a", T.stg2[64, 0:8], T.th[:], "", "stg2", "dstg2")
-    dma("s", T.stg2[65:128, :], T.mem[:, 0:126], "", "stg2", "dstg2")
-    dma("a", T.stg2[64, 8:16], T.th[:], "", "stg2", "dstg2")
-    dma("s", T.lnd[me, 0:64, :], T.col[mine, :], "", "own", "down")
-    dma("a", T.lnd[me, 64:128, :], T.om[mine, :], "", "own", "down")
-    dma("s", T.lnd2[me, 8 * me:8 * me + 8, :], T.mem[me, :], "", "own", "down")
-    dma("a", T.lnd2[me, 64, 0:8], T.th[:], "", "own", "down")
-    iota(T.pc[:, 0:1], [[0, 1]], 0, 1, "pc0", 1)
+    dma("s", T.stg[:, 0:64, :], T.col[:], "", "stg ~s0", "dstg")
+    dma("a", T.stg[:, 64:128, :], T.om[:], "", "stg ~a0", "dstg")
+    dma("s", T.stg2[:, 0:64, :], T.mem[:], "", "stg2 ~s0", "dstg2")
+    dma("a", T.stg2[:, 64:128, :], T.mem[:], "", "stg2 ~a0", "dstg2")
+    dma("s", T.stg3[0:4, :], T.th[:], "", "stg2 ~s0", "dstg2")
+    dma("a", T.stg3[4:128, :], T.mem[0:2, 0:124], "", "stg2 ~a0", "dstg2")
+    dma("s", T.lnd[me, 0:64, :], T.col[mine, :], "", "own ~s0", "down")
+    dma("a", T.lnd[me, 64:128, :], T.om[mine, :], "", "own ~a0", "down")
+    dma("s", T.lnd2[me, 0:64, :], T.mem[me, :], "", "own2 ~s0", "down2")
+    dma("a", T.lnd3[me, 0:4, :], T.th[:], "", "own2 ~a0", "down2")
     iota(T.i1[:], [[-1, 128]], 128, 1, "i1", 128)
-    iota(T.j2[:], [[1, 8], [0, 16]], 0, 0, "j2", 128)
-    iota(T.r8[:], [[1, 8]], 0, 0, "r8", 8)
     iota(T.b0[:], [[77, 4], [80, 8]], 0, 5, "b0", 32)
-    iota(T.li[:], [[1, 128]], 0, 0, "li", 128)
     exchange(lambda r: T.stg[r], T.lnd[me], "stg", "arr1", "lnd")
-    exchange(lambda r: T.stg2[:], T.lnd2[me], "stg2", "arr2", "lnd2")
-    dma("s", T.cc[:], T.lnd[:, 0:64, :], "lnd own", "cc", "dcc")
-    dma("a", T.oo[:], T.lnd[:, 64:128, :], "lnd own", "oo", "doo")
-    dma("s", T.memr[0:8, :], T.lnd2[:, 8 * me:8 * me + 8, :], "lnd2 own", "memr", "dmem")
-    dma("s", T.th8[0:8, :], T.lnd2[:, 64, 0:8], "lnd2 own", "th8", "dth")
+    exchange(lambda r: T.stg2[r], T.lnd2[me], "stg2", "arr2", "lnd2", (T.stg3[:], T.lnd3[me], "arr3", "lnd3"))
+    dma("s", T.cc[:], T.lnd[:, 0:64, :], "lnd own", "cc ~s0", "dcc")
+    dma("s", T.oo[:], T.lnd[:, 64:128, :], "lnd own", "oo ~s0", "doo")
+    dma("s", T.memr[0:8, :], T.lnd2[:, 0:64, :], "lnd2 own2", "memr ~s0", "dmem")
+    dma("s", T.th8[0:8, :], T.lnd3[:, 0:4, :], "lnd3 own2", "th8 ~s0", "dth")
 
     fill(T.b61[:], 0.0, "", "b61z", 124)
     fill(T.keep[:], 1.0, "", "keep0", 128)
     fill(T.vt[:, 1024:4104:1024], -3000.0, "", "vt0")
     fill(T.keep[:, 0:256:16], 0.0, "keep0", "keep")
+    t1(T.pc[:, 0:1], T.i1[:, 0:1], -128.0, A.add, "i1", "pc0", 1)
+    cp(T.pf[:, 5:6], T.i1[:, 0:1], "i1", "pf5", 1)
+    ts(T.li[:], T.i1[:], -1.0, T.pf[:, 5:6], A.mult, A.add, "i1 pf5", "li")
+    t1(T.j2[:], T.li[:], 4, A.arith_shift_right, "li", "j2")
     t1(T.b0f[:], T.i1[:, 0:64], 0.0, A.mult, "i1", "b0f", 64)
     t1(T.pc[:, 1:2], T.pc[:, 0:1], 4, A.arith_shift_right, "pc0", "pc1", 1)
     t1(T.pc[:, 2:3], T.pc[:, 0:1], 15, A.bitwise_and, "pc0", "pc2", 1)
@@ -303,7 +339,7 @@ def rank_program(g, core, T, topo):
     t1(T.idn[:], T.i1[:], 128.0, A.is_equal, "i1", "idn")
     cp(T.pf[:, 0:3], T.pc[:, 0:3], "pc0 pc1 pc2", "pf", 3)
     t1(T.am[:], T.i1m[:], 0.0, A.is_equal, "i1m", "am")
-    t1(T.mr[:], T.r8[:], T.pf[:, 1:2], A.is_equal, "r8 pf", "mr", 8)
+    t1(T.mr[:], T.li[:, 0:8], T.pf[:, 1:2], A.is_equal, "li pf", "mr", 8)
     t1(T.pf[:, 3:4], T.pf[:, 1:2], 48.0, A.mult, "pf", "pf3", 1)
     t1(T.pf[:, 4:5], T.pf[:, 1:2], 128.0, A.mult, "pf", "pf4", 1)
     t1(T.g8[0:8, :], T.j2[0:8, :], T.pf[0:8, 0:1], A.is_equal, "j2 pf", "g8")
@@ -338,6 +374,7 @@ def rank_program(g, core, T, topo):
             mmul(T[b][:, c:c + 128], mats[:, 128 * r:128 * r + 128], T[name][:],
                  start is True or (start == "first" and r % 4 == 0),
                  stop is True or (stop == "last" and r % 4 == 3), name + mname, b + " ~" + b[:2])
+        join(4)
 
     def table(dst, c0, b, name):
         act(dst[:, c0:c0 + 512], T[b][:], b, name, busy=0.56)
@@ -361,9 +398,9 @@ def rank_program(g, core, T, topo):
     mmul(T.py[:, 0:128], T.idn[:], T.tq[:], False, True, "idn tq", "py")
     cp(T.memf[0:8, 128:136], T.th8[0:8, :], "th8", "memf1", 8)
     tt(T.xs[:], T.x16[:], T.py[:, 0:128], A.max, "py x16", "xs")
-    mmul(T.px[:, 128:136], T.g8[0:8, :], T.memf[0:8, 128:136], True, True, "g8 memf1", "px", 64)
     ts(T.onep[:], T.tq[:], 0.125, 1024.0, A.mult, A.add, "tq", "onep", 64)
     mmul(T.px[:, 256:384], T.idn[:], T.onep[:], True, True, "idn onep", "px")
+    mmul(T.px[:, 128:136], T.g8[0:8, :], T.memf[0:8, 128:136], True, True, "g8 memf1", "px", 64)
     cp(T.thc[:, 0:1], T.px[:, 128 + me:129 + me], "px", "thc0", 1)
     t1(T.onen[:], T.onep[:], -1.0, A.mult, "onep", "onen", 64)
     tt(T.t3[:], T.tq[:], T.lanec[:], A.subtract, "tq lanec", "t3", 256)
@@ -372,8 +409,9 @@ def rank_program(g, core, T, topo):
     t1(T.t4[:], T.onep[:], 8.0, A.mult, "onep", "t4")
     tt(T.oe3[:], T.t4[:], T.lane3[:], A.min, "t4 lane3", "oe3", 256)
 
-    ends = [0, 16, 48, 80, 112, 128]
-    sums = {1: (0, 48), 3: (48, 112)}
+    ends = [0, 24, 56, 88, 112, 128]
+    sums = {1: (0, 56), 3: (56, 112)}
+    share = 8
     vts = " vt0"
     for t in range(4):
         last = t == 3
@@ -389,6 +427,10 @@ def rank_program(g, core, T, topo):
         ts(T.off[:], x[:], B - 2048.0, 2048.0, A.min, A.add, xn, "off", 128 if last else 64)
         for c in range(5):
             lo, hi = ends[c], ends[c + 1]
+            if c == 3:
+                cp(T.gb[:, 16 * lo:16 * (lo + share)], T.vt[:, 0:B + 1].indirect(T.off[:, lo:lo + share]), "off" + vts, "gd",
+                   20 + 25 * share)
+                lo += share
             act(T.gb[:, 16 * lo:16 * hi], T.vt[:, 0:B + 1].indirect(T.off[:, lo:hi]), "off" + vts, "gb%d ~gb" % c,
                 busy=0.06 + 0.025 * (hi - lo))
         own = "z16" if t == 0 else "ownk"
@@ -401,11 +443,9 @@ def rank_program(g, core, T, topo):
         mmul(low, T.lowt[:], T.idn[:], True, True, "lowt idn", "py")
         if last:
             t1(T.xo[:], T.xf[:], 2048.0, A.add, "xf", "xo")
-            dma("s", T.stgw[:, 80:128, :], T.lane3[:, 0:96], "lane3 xf", "pad", "dpad")
-            dma("s", T.stgx[:], T.xo[:], "xo", "stgx", "dx")
-            dma("s", T.lndx[me], T.xo[mine, :], "xo", "ownx", "dxo")
+            dma("s", T.stgx[:], T.xo[:], "xo", "stgx ~s0", "dx")
+            dma("s", T.lndx[me], T.xo[mine, :], "xo", "ownx ~s0", "dxo")
             exchange(lambda r: T.stgx[r], T.lndx[me], "stgx", "arrx", "lndx")
-            dma("s", T.yx[:], T.lndx[:], "lndx ownx", "", "dy")
             t1(T.t2[:], low, 3500.0, A.is_lt, "py", "t2")
             t1(T.pv0[:, 0:128], low, 2048.0, A.add, "py", "pv0")
             tt(T.pv1[:, 0:128], T.t2[:], T.pv0[:, 0:128], A.mult, "t2 pv0", "pv1")
@@ -426,7 +466,8 @@ def rank_program(g, core, T, topo):
             b = "pe%d" % (c % 2)
             w = 16 * (hi - lo)
             mmul(T[b][:, 0:w], T.lowt[:], T.ex[:, 16 * lo:16 * hi], True, True, "lowt" + exs, b + " ~ex", w)
-            tt(T.f1[:, 16 * lo:16 * hi], T.gb[:, 16 * lo:16 * hi], T[b][:, 0:w], A.is_ge, "gb%d %s" % (c, b), "f1_%d ~f1" % c, w)
+            tt(T.f1[:, 16 * lo:16 * hi], T.gb[:, 16 * lo:16 * hi], T[b][:, 0:w], A.is_ge,
+               "gb%d %s" % (c, b) + (" gd" if c == 3 else ""), "f1_%d ~f1" % c, w)
             if c in sums:
                 l0, l1 = sums[c]
                 if c == 3:
@@ -435,6 +476,8 @@ def rank_program(g, core, T, topo):
                 for k in range(16):
                     mmul(T.px[:, l0:l1], T.idb[:], T.f1[:, 16 * l0 + k:16 * l1:16], c == 1 and k == 0, False,
                          "idb f1_%d f1_%d" % (c - 1, c), "px", 64)
+                    if k % 4 == 3:
+                        join(4)
         op("v", lambda: V.tensor_tensor_scan(T.sc[:], T.keep[:], T.f1[:, 1792:2048], 0.0, A.mult, A.add), "keep f1_4", "sc")
         mmul(T.px[:, 112:128], T.idb[:], T.sc[:, 15:256:16], False, True, "idb sc", "px", 64)
         if t > 0:
@@ -448,6 +491,7 @@ def rank_program(g, core, T, topo):
             mmul(T.px[:, 0:16], T.idn[:], T.b0f[:, 16 * (t + 1):16 * (t + 2)], True, False, "idn b0f%d" % (t + 1), "px", 64)
             for a in range(16):
                 mmul(T.px[:, 0:16], T.dg[:, 128 * a:128 * a + 128], T.ft[:, a:256:16], False, a == 15, "ft0 ft1" + dgs, "px", 64)
+            join(16)
         t1(T.up[:], T.py[:, 0:128], T.thc[:, 0:1], A.is_ge, "py thc0", "up")
         tt(T.mm[:], T.py[:, 128:256], T.up[:], A.mult, "py up", "mm")
         if last:
@@ -472,11 +516,13 @@ def rank_program(g, core, T, topo):
         cp(T.o16[:], T.oj[:], "oj", "o16", 16)
 
     rs = names("rh", 4)
-    dma("a", T.stgw[:, 64:80, :], T.rh[0:128:16, :], rs, "stgw", "dw")
-    dma("s", T.stgw[:, 0:64, :], T.wo[:], "wo", "stgw", "dw")
-    dma("a", T.lndw[me, 64:80, :], T.rh[16 * me:16 * me + 1, :], rs, "ownw", "dwo")
-    dma("s", T.lndw[me, 0:64, :], T.wo[mine, :], "wo", "ownw", "dwo")
-    exchange(lambda r: T.stgw[r], T.lndw[me], "stgw pad", "arrw", "lndw")
-    dma("s", T.yo[:], T.lndw[:, 0:64, :], "lndw ownw", "", "dyo")
-    dma("a", T.yr[:], T.lndw[:, 64:80, :], "lndw ownw", "", "dyr")
+    dma("s", T.stgw[:], T.wo[:], "wo", "stgw ~s0", "dw")
+    dma("a", T.stgr[:], T.rh[0:128:16, :], rs, "stgr", "dr")
+    dma("s", T.lndw[me], T.wo[mine, :], "wo", "ownw ~s0", "dwo")
+    dma("a", T.lndr[me], T.rh[16 * me:16 * me + 1, :], rs, "ownr", "dro")
+    dma("s", T.yx[:], T.lndx[:], "lndx ownx", "~s0", "dy")
+    exchange(lambda r: T.stgw[r], T.lndw[me], "stgw", "arrw", "lndw")
+    exchange(lambda r: T.stgr[r], T.lndr[me], "stgr", "arrr", "lndr")
+    dma("s", T.yo[:], T.lndw[:], "lndw ownw", "~s0", "dyo")
+    dma("a", T.yr[:], T.lndr[:], "lndr ownr", "", "dyr")
     emit(ops, g, T, arrivals)

@@ -2,42 +2,43 @@ from concourse.bass import DstId, RemoteDMATransfer
 from concourse.mybir import AluOpType as A
 from concourse.mybir import ActivationFunctionType as AF
 
-H, F, BF, I, U = "float16", "float32", "bfloat16", "int32", "uint16"
-PSUM = ("pv0", "pv1", "pk0", "pk1", "pe0", "pe1", "px", "py")
-SCRATCH = {
-    "stg": ("dram", [8, 128, 32], I), "lnd": ("dram", [8, 128, 32], I),
-    "stg2": ("dram", [8, 128, 2], I), "lnd2": ("dram", [8, 128, 2], I),
-    "stg3": ("dram", [128, 2], I), "lnd3": ("dram", [8, 128, 2], I),
-    "stgx": ("dram", [8, 128, 16], F), "lndx": ("dram", [8, 128, 16], F),
-    "stgw": ("dram", [8, 128, 16], F), "lndw": ("dram", [8, 128, 16], F),
-    "stgr": ("dram", [8, 128, 4], F), "lndr": ("dram", [8, 128, 4], F),
-}
+H, F, I, U = "float16", "float32", "int32", "uint16"
+PSUM = ("pa", "pb", "pk0", "pk1", "pe0", "pe1", "pc0", "pc1")
+SCRATCH = {"stgt": ("dram", [128, 2], I), "lndt": ("dram", [8, 128, 2], I)}
+for _n, _w, _dt in (("c", 16, I), ("m", 2, I), ("o", 16, I), ("x", 16, F), ("w", 16, F), ("r", 4, F)):
+    SCRATCH["stg" + _n] = ("dram", [8, 128, _w], _dt)
+    SCRATCH["lnd" + _n] = ("dram", [8, 128, _w], _dt)
 for _dt, _w, _names in (
-        (I, 128, "i1 i1m j2 li cc oo memr"), (I, 8, "pc th8"), (I, 32, "b0"), (I, 16, "oi oj"),
+        (I, 128, "i1 i1m j2 li ln b0 cc oo memr sc"), (I, 8, "pi th8"), (I, 16, "oj"),
         (U, 128, "off"), (U, 16, "o16"),
-        (F, 8, "pf mr mrk thc tu tv"), (F, 128, "nid lane3 xf xs x1 xo k1 k2 ownk mm t2 t3 t4 oe3 wo"),
-        (F, 512, "rh"), (F, 1024, "kt"), (F, 2048, "gb"), (F, 4104, "vt"),
-        (H, 64, "b0f"), (H, 128, "idn am g8 lanec x16 t8 lowt z16 ta tb tq onep onen zb"), (H, 136, "memf"),
-        (H, 1024, "sel"), (H, 2048, "ex"),
-        (BF, 128, "idb idk amb blk sf up"), (BF, 248, "b61"), (BF, 256, "keep sc ft"), (BF, 1024, "selk"),
-        (BF, 2048, "dg f1")):
+        (F, 8, "mr thc"), (F, 16, "pf"), (F, 128, "xf xs x1 xo k1 k2 ownk mm wo rc yi"), (F, 2048, "kt"), (F, 4104, "vt"),
+        (H, 128, "c2k idn idq ndq nid idh id9 am blk b61 g8 mneg lanec x16 om16 low0 low z16 tq onep zb sf ft t2 yc y0 keep"),
+        (H, 128, "lr"), (H, 136, "memf"), (H, 512, "t8 up cst"), (H, 1024, "sel"), (H, 2048, "f1 gb")):
     for _n in _names.split():
         SCRATCH[_n] = ("sbuf", [128, _w], _dt)
 for _n in PSUM:
     SCRATCH[_n] = ("psum", [128, 512], F)
-SEMAPHORES = ["g", "v", "a", "p", "dstg", "dstg2", "down", "down2", "dcc", "doo", "dmem", "dth", "dx", "dxo", "dw", "dwo",
-              "dr", "dro", "dy", "dyo", "dyr", "arr1", "arr2", "arr3", "arrx", "arrw", "arrr", "sent"]
+SEMAPHORES = ["g", "v", "a", "p", "sent", "arrt", "ldt"] + [a + b for a in ("put", "own", "arr", "ld") for b in "cmoxwr"]
 MAGIC = 1.5 * 2.0 ** 36
-HOP = 0.06
-SPEEDS = (({}, HOP), ({"a": 1.25}, HOP), ({"p": 1.4}, HOP), ({"v": 1.15, "a": 0.8}, HOP), ({}, 2.5 * HOP))
-ORDER = {}
+PIECES = ((0, 32), (32, 64))
+
+ORDER = """
+s.e1< l.x11< mm0> *kz1> s.*mem< oj1> s.onep l.off0 l.*mark1 x11 kt0> l.ga1 ga1 l.fb0 s.kt0 x10 x161 *fb0> s.*one0 fd0>
+s.*one1 l.fa0 l.k21 s.kt1 *y0> o161> *kz0> l.off1 l.sf0< *S0> ownk1> *d0> s.*kt0 t80 l.*fd0 x160 s.xs0< l.*S0 s.*zb
+ft1 *yS0> *kT1 l.*g1 k11 up0 *own0> l.*fd1 oj0 l.*gl1 *fd0 l.xo0 *kup0> off0 s.thc2 *vt1 s.*vt1< l.gb1 k21 s.x161<
+l.k20 k10 l.t81 gb1 s.thc0 ga0 s.thc1 s.memf< gb0 l.fb1 vt1 t81 l.t80 k20 s.e0< l.gb0 l.ga0 l.low1 sf1 s.x160< s.vt1<
+l.low0 low0 fa1 l.t21 s.zb l.k11< l.fc0 l.xo1 l.*low1< l.t20 l.rc1< l.fa1 *fd1 l.fd1 l.sf1 up1 l.*fc1 *fb1 off1< fb1
+l.fc1 l.*low0 o160 *sf1< *fa0 *d1 s.*kt1< *low0< z160 l.*fc0 fc1 fd1 xs1 sc1 l.*sf0 s.*vt0< sc0 *kT0< l.ft1 l.rc0 *sf0
+fa0 l.*gl0 z161 *fa1< fc0 fb0 l.*fa1 ft0 s.vt0< vt0 kt1< *S1 sf0 l.*g0 l.xf0< *yup1 *low1< l.*mark0< mm1 s.tq< s.thf<
+s.pe0< l.*fb0 l.k10< *vt0 xs0< l.*sf1 l.*fb1 *fc1< l.up0 s.om16< l.fd0 s.*e< s.*th< l.*Rup0 *y1< *fc0 l.xf1< l.*fa0
+*yS1 ownk0 l.x10< l.*S1 *own1 *kup1 *yup0 l.*R1 low1< s.low0< l.up1 l.ft0 l.*Rup1 l.mm1 l.*R0 l.*mup1 l.mm0 l.*mup0
+l.wo1 l.wo0
+"""
 
 
 def needs(ops):
     writer, readers, deps, follow, lines = {}, {}, [], [], {}
-    for k, (q, fn, rd, wr, sem, busy, lat) in enumerate(ops):
-        line = [w for w in wr if w[0] == "~"]
-        wr = [w for w in wr if w[0] != "~"]
+    for k, (q, fn, rd, wr, sem, busy, lat, t, tag) in enumerate(ops):
         d = set()
         for r in rd:
             d.update(writer.get(r, []))
@@ -50,9 +51,9 @@ def needs(ops):
         if q == "p":
             f = set(x for x in d if ops[x][0] == "p")
             d -= f
-        for name in line:
-            f.update(lines.get(name, []))
-            lines[name] = [k]
+        if sem is not None and fn is not None:
+            f.update(lines.get(q, []))
+            lines[q] = [k]
         for r in rd:
             readers.setdefault(r, []).append(k)
         for w in wr:
@@ -69,96 +70,16 @@ def needs(ops):
     return deps, follow
 
 
-def place(ops, deps, follow, rank):
-    n = len(ops)
-    start, slots = [0.0] * n, {}
-    for k in sorted(range(n), key=lambda i: (-rank[i], i)):
-        q, busy = ops[k][0], ops[k][5]
-        s = max([0.0] + [start[x] + ops[x][6] + HOP for x in deps[k]] + [start[x] + ops[x][5] for x in follow[k]])
-        lst = slots.setdefault(q, [])
-        at = len(lst)
-        for i in range(len(lst)):
-            a, b = lst[i]
-            if b <= s:
-                continue
-            if s + busy <= a:
-                at = i
-                break
-            s = b
-        lst.insert(at, (s, s + busy))
-        start[k] = s
-    return sorted(range(n), key=lambda i: (start[i], i))
-
-
-def span(ops, deps, order, which):
-    speed, hop = SPEEDS[which]
-    free, last, end, held = {}, {}, {}, {}
-    for k in order:
-        q = ops[k][0]
-        f = speed.get(q, 1.0) if ops[k][4] is None else 1.0
-        s, by = free.get(q, 0.0), last.get(q)
-        for x in deps[k]:
-            if end[x] + hop > s:
-                s, by = end[x] + hop, x
-        free[q] = s + ops[k][5] * f
-        last[q] = k
-        end[k] = s + ops[k][6] * f
-        held[k] = by
-    k = max(end, key=end.get)
-    return end[k], held, k
-
-
 def arrange(ops, deps, follow):
-    n = len(ops)
-    if n in ORDER:
-        return ORDER[n]
-    seed = [12345]
-
-    def draw():
-        seed[0] = (seed[0] * 6364136223846793005 + 1442695040888963407) % 2 ** 64
-        return (seed[0] >> 11) / 2.0 ** 53
-
-    first = min(k for k in range(n) if "cc" in ops[k][2])
-    rank = [0.0] * n
-    for k in range(n - 1, -1, -1):
-        rank[k] += ops[k][6] + (60.0 if k < first and ops[k][4] is None else 0.0)
-        for x in deps[k]:
-            rank[x] = max(rank[x], rank[k] + HOP)
-        for x in follow[k]:
-            rank[x] = max(rank[x], rank[k])
-    order = place(ops, deps, follow, rank)
-    before = [deps[k] | follow[k] for k in range(n)]
-    runs = [span(ops, deps, order, w) for w in range(len(SPEEDS))]
-    cost = sum(r[0] for r in runs)
-    best, kept, steps = cost, order, 9000
-    for it in range(steps):
-        _, held, k = runs[int(draw() * len(runs))]
-        pairs = []
-        while held[k] is not None:
-            if ops[held[k]][0] == ops[k][0] and held[k] not in before[k]:
-                pairs.append((held[k], k))
-            k = held[k]
-        if not pairs:
-            break
-        j, k = pairs[int(draw() * len(pairs))]
-        a, b = order.index(j), order.index(k)
-        behind, rest = {j}, []
-        for x in order[a + 1:b + 1]:
-            if before[x] & behind:
-                behind.add(x)
-            else:
-                rest.append(x)
-        if k in behind:
-            continue
-        o = order[:a] + rest + [x for x in order[a:b + 1] if x in behind] + order[b + 1:]
-        rs = [span(ops, deps, o, w) for w in range(len(SPEEDS))]
-        v = sum(r[0] for r in rs)
-        if v <= cost + 0.6 * draw() * (1.0 - it / steps):
-            cost, order, runs = v, o, rs
-            if v < best:
-                best, kept = v, o
-    ORDER[n] = kept
-    return kept
+    place = {name.strip("<>"): (name.count(">") - name.count("<"), n) for n, name in enumerate(ORDER.split())}
+    key = [(max(o[7], 0) + place[o[8]][0], place[o[8]][1]) if o[8] in place else (-9, k) for k, o in enumerate(ops)]
+    done, order, left = set(), [], sorted(range(len(ops)), key=lambda k: key[k])
+    while left:
+        k = next(k for k in left if (deps[k] | follow[k]) <= done)
+        left.remove(k)
+        done.add(k)
+        order.append(k)
+    return order
 
 
 def emit(ops, g, T, arrivals):
@@ -208,7 +129,7 @@ def emit(ops, g, T, arrivals):
             total[src] = 16 * count[src]
     waited = {}
     for k in order:
-        q, fn, rd, wr, sem, busy, lat = ops[k]
+        q, fn, rd, wr, sem = ops[k][:5]
         for src, x in waits[k]:
             c = val[x] if ops[x][4] is None else total[src]
             queues[q].wait_ge(T.sem[src], c)
@@ -233,296 +154,307 @@ def rank_program(g, core, T, topo):
     cores = list(T.cores)
     others = [r for r in range(8) if r != me]
     V, S, P = g.vector, g.scalar, g.tensor
-    ops = []
+    ops, now = [], [-2]
 
-    def op(q, fn, rd, wr, sem=None, busy=0.16, lat=None):
-        ops.append((q, fn, rd.split(), wr.split(), sem, busy, busy if lat is None else lat))
+    def op(q, fn, rd, wr, busy, sem=None, lat=None, tag=None):
+        tag = {-2: "c.", -1: "s.", 3: "l."}.get(now[0], "") + (tag or wr.split()[0].split("@")[0])
+        ops.append((q, fn, rd.split(), wr.split(), sem, busy, busy if lat is None else lat, now[0], tag))
 
-    def vt_(n):
+    def cost(n):
         return 0.03 + 0.001 * max(64, n)
 
-    def ts(out, in0, s1, s2, op0, op1, rd, wr, n=128):
-        if s2 is None:
-            op("v", lambda: V.tensor_scalar(out, in0, s1, None, op0), rd, wr, busy=vt_(n))
-        else:
-            op("v", lambda: V.tensor_scalar(out, in0, s1, s2, op0, op1), rd, wr, busy=vt_(n))
+    def ts(out, in0, s1, s2, op0, op1, rd, wr, n=64):
+        op("v", lambda: V.tensor_scalar(out, in0, s1, s2, op0, op1), rd, wr, cost(n))
 
-    def t1(out, in0, s1, op0, rd, wr, n=128):
-        ts(out, in0, s1, None, op0, None, rd, wr, n)
+    def t1(out, in0, s1, op0, rd, wr, n=64):
+        op("v", lambda: V.tensor_scalar(out, in0, s1, None, op0), rd, wr, cost(n))
 
-    def tt(out, in0, in1, o, rd, wr, n=128):
-        op("v", lambda: V.tensor_tensor(out, in0, in1, o), rd, wr, busy=vt_(n))
+    def tt(out, in0, in1, o, rd, wr, n=64):
+        op("v", lambda: V.tensor_tensor(out, in0, in1, o), rd, wr, cost(n))
 
-    def cp(out, in_, rd, wr, n=128):
-        op("v", lambda: V.tensor_copy(out, in_), rd, wr, busy=vt_(n))
+    def cp(out, in_, rd, wr, n=64):
+        op("v", lambda: V.tensor_copy(out, in_), rd, wr, cost(n))
 
     def fill(out, c, rd, wr, n=64):
-        op("v", lambda: V.memset(out, c), rd, wr, busy=vt_(n))
+        op("v", lambda: V.memset(out, c), rd, wr, cost(n))
 
-    def act(out, in_, rd, wr, scale=None, busy=0.17):
-        if scale is None:
-            op("a", lambda: S.activation(out, in_, AF.Copy), rd, wr, busy=busy)
-        else:
-            op("a", lambda: S.activation(out, in_, AF.Copy, scale=scale), rd, wr, busy=busy)
+    def act(out, in_, rd, wr, n=64, scale=1.0):
+        op("a", lambda: S.activation(out, in_, AF.Copy, scale=scale), rd, wr, 0.02 + cost(n))
 
-    def mmul(out, lhs, rhs, start, stop, rd, wr, n=128):
-        op("p", lambda: P.matmul(out, lhs, rhs, start, stop), rd, wr, busy=0.0005 * max(64, n))
+    def fn(out, in_, f, bias, scale, rd, wr, n=64, tag=None):
+        op("a", lambda: S.activation(out, in_, f, bias=bias, scale=scale), rd, wr, 0.02 + cost(n), tag=tag)
 
-    def join(n):
-        part = ops[-n:]
-        del ops[-n:]
-        busy = sum(x[5] for x in part)
-        ops.append(("p", lambda: [x[1]() for x in part][-1], sum((x[2] for x in part), []), part[0][3], None, busy, busy))
+    def mmul(tag, b, terms, start=True, stop=True, n=64):
+        def run():
+            for k, x in enumerate(terms):
+                each = start == "each"
+                ins = P.matmul(x[0], x[1], x[2], each or (start and k == 0), each or (stop and k == len(terms) - 1))
+            return ins
+        op("p", run, " ".join(x[3] for x in terms), b, 0.0005 * max(64, n) * len(terms), tag="*" + tag)
 
     def dma(q, out, in_, rd, wr, sem):
         eng = g.sync if q == "s" else g.scalar
-        op(q, lambda: eng.dma_start(out, in_), rd, wr, sem, 0.08, 2.3)
+        op(q, lambda: eng.dma_start(out, in_), rd, wr, 0.08, sem, 1.9 if sem in ("putr", "ldr", "ldm", "ldt") else 2.3, "dma")
 
-    def iota(out, pattern, base, cm, name, n):
-        op("g", lambda: g.iota(out, pattern, base, cm), "", name, busy=0.13 + 0.002 * n)
+    def iota(out, pattern, base, cm, name):
+        op("g", lambda: g.iota(out, pattern, base, cm), "", name, 0.39)
 
     def names(stem, n):
         return " " + " ".join(stem + str(k) for k in range(n))
 
-    def exchange(src, dst, rd, arr, name, common=None):
+    arrivals = {"arr" + x: len(others) for x in "cmotxwr"}
+    arrivals["sent"] = 0
+
+    def exchange(x, common=""):
         trs, ids, used, free = [], [], 0, -1
         for r in others:
             rid, pid = topo.addr(cores[r], core)
             ids.append(DstId(rid=rid, pnc=pid))
-            e = [x for x in topo.engines(core, cores[r]) if not used >> x & 1][0]
+            e = [n for n in topo.engines(core, cores[r]) if not used >> n & 1][0]
             used |= 1 << e
             free &= topo.mask(core, cores[r])
-            trs.append(RemoteDMATransfer(dst_ids=[ids[-1]], dma_engine_mask=1 << e, remote_sem=T.sem[arr], src=src(r), dst=dst))
-        if common is not None:
+            trs.append(RemoteDMATransfer(dst_ids=[ids[-1]], dma_engine_mask=1 << e, remote_sem=T.sem["arr" + x],
+                                         src=T["stg" + x][r], dst=T["lnd" + x][me]))
+        if common:
             free &= ~used
-            trs.append(RemoteDMATransfer(dst_ids=ids, dma_engine_mask=free & -free, remote_sem=T.sem[common[2]],
-                                         src=common[0], dsts=[common[1]] * len(ids)))
-        op("g", lambda: g.remote_dma_fused(trs, local_sem=T.sem.sent), rd, "~calls call" + arr, "sent", 0.5, 3.5)
-        op("n", None, "call" + arr, name, arr, 0.0, 0.001)
-        if common is not None:
-            op("n", None, "call" + arr, common[3], common[2], 0.0, 0.001)
+            trs.append(RemoteDMATransfer(dst_ids=ids, dma_engine_mask=free & -free, remote_sem=T.sem["arr" + common],
+                                         src=T["stg" + common][:], dsts=[T["lnd" + common][me]] * len(ids)))
+        arrivals["sent"] += len(trs)
+        op("g", lambda: g.remote_dma_fused(trs, local_sem=T.sem.sent), "stg" + x, "call" + x, 0.5, "sent", 3.5)
+        for y in x + common:
+            op("n", None, "call" + x, "lnd" + y, 0.0, "arr" + y, 0.001)
 
-    arrivals = {"arr1": 7, "arr2": 7, "arr3": 7, "arrx": 7, "arrw": 7, "arrr": 7, "sent": 36}
     mine = slice(16 * me, 16 * me + 16)
+    both = (1, 0)
 
-    dma("s", T.stg[:, 0:64, :], T.col[:], "", "stg ~s0", "dstg")
-    dma("a", T.stg[:, 64:128, :], T.om[:], "", "stg ~a0", "dstg")
-    dma("s", T.stg2[:, 0:64, :], T.mem[:], "", "stg2 ~s0", "dstg2")
-    dma("a", T.stg2[:, 64:128, :], T.mem[:], "", "stg2 ~a0", "dstg2")
-    dma("s", T.stg3[0:4, :], T.th[:], "", "stg2 ~s0", "dstg2")
-    dma("a", T.stg3[4:128, :], T.mem[0:2, 0:124], "", "stg2 ~a0", "dstg2")
-    dma("s", T.lnd[me, 0:64, :], T.col[mine, :], "", "own ~s0", "down")
-    dma("a", T.lnd[me, 64:128, :], T.om[mine, :], "", "own ~a0", "down")
-    dma("s", T.lnd2[me, 0:64, :], T.mem[me, :], "", "own2 ~s0", "down2")
-    dma("a", T.lnd3[me, 0:4, :], T.th[:], "", "own2 ~a0", "down2")
-    iota(T.i1[:], [[-1, 128]], 128, 1, "i1", 128)
-    iota(T.b0[:], [[77, 4], [80, 8]], 0, 5, "b0", 32)
-    exchange(lambda r: T.stg[r], T.lnd[me], "stg", "arr1", "lnd")
-    exchange(lambda r: T.stg2[r], T.lnd2[me], "stg2", "arr2", "lnd2", (T.stg3[:], T.lnd3[me], "arr3", "lnd3"))
-    dma("s", T.cc[:], T.lnd[:, 0:64, :], "lnd own", "cc ~s0", "dcc")
-    dma("s", T.oo[:], T.lnd[:, 64:128, :], "lnd own", "oo ~s0", "doo")
-    dma("s", T.memr[0:8, :], T.lnd2[:, 0:64, :], "lnd2 own2", "memr ~s0", "dmem")
-    dma("s", T.th8[0:8, :], T.lnd3[:, 0:4, :], "lnd3 own2", "th8 ~s0", "dth")
+    def half(h, at=0, w=64):
+        return slice(at + w * h, at + w * h + w)
 
-    fill(T.b61[:], 0.0, "", "b61z", 124)
-    fill(T.keep[:], 1.0, "", "keep0", 128)
-    fill(T.vt[:, 1024:4104:1024], -3000.0, "", "vt0")
-    fill(T.keep[:, 0:256:16], 0.0, "keep0", "keep")
-    t1(T.pc[:, 0:1], T.i1[:, 0:1], -128.0, A.add, "i1", "pc0", 1)
-    cp(T.pf[:, 5:6], T.i1[:, 0:1], "i1", "pf5", 1)
-    ts(T.li[:], T.i1[:], -1.0, T.pf[:, 5:6], A.mult, A.add, "i1 pf5", "li")
-    t1(T.j2[:], T.li[:], 4, A.arith_shift_right, "li", "j2")
-    t1(T.b0f[:], T.i1[:, 0:64], 0.0, A.mult, "i1", "b0f", 64)
-    t1(T.pc[:, 1:2], T.pc[:, 0:1], 4, A.arith_shift_right, "pc0", "pc1", 1)
-    t1(T.pc[:, 2:3], T.pc[:, 0:1], 15, A.bitwise_and, "pc0", "pc2", 1)
-    t1(T.i1m[:], T.i1[:], 15, A.bitwise_and, "i1", "i1m")
-    t1(T.idn[:], T.i1[:], 128.0, A.is_equal, "i1", "idn")
-    cp(T.pf[:, 0:3], T.pc[:, 0:3], "pc0 pc1 pc2", "pf", 3)
-    t1(T.am[:], T.i1m[:], 0.0, A.is_equal, "i1m", "am")
-    t1(T.mr[:], T.li[:, 0:8], T.pf[:, 1:2], A.is_equal, "li pf", "mr", 8)
-    t1(T.pf[:, 3:4], T.pf[:, 1:2], 48.0, A.mult, "pf", "pf3", 1)
-    t1(T.pf[:, 4:5], T.pf[:, 1:2], 128.0, A.mult, "pf", "pf4", 1)
-    t1(T.g8[0:8, :], T.j2[0:8, :], T.pf[0:8, 0:1], A.is_equal, "j2 pf", "g8")
+    dma("s", T.stgc[:], T.col[:], "", "stgc", "putc")
+    dma("a", T.stgm[:, 0:64, :], T.mem[:], "", "stgm", "putm")
+    dma("s", T.stgm[:, 64:128, :], T.mem[:], "", "stgm", "putm")
+    dma("a", T.stgt[0:4, :], T.th[:], "", "stgm", "putm")
+    dma("s", T.stgt[4:128, :], T.mem[0:2, 0:124], "", "stgm", "putm")
+    dma("a", T.stgo[:], T.om[:], "", "stgo", "puto")
+    dma("s", T.lndc[me], T.col[mine, :], "", "ownc", "ownc")
+    dma("a", T.lndo[me], T.om[mine, :], "", "owno", "owno")
+    dma("s", T.lndm[me, 0:64, :], T.mem[me, :], "", "ownm", "ownm")
+    dma("a", T.lndt[me, 0:4, :], T.th[:], "", "ownm", "ownm")
+    iota(T.i1[:], [[-1, 128]], 128, 1, "i1")
+    iota(T.ln[:], [[1, 2], [2, 64]], -1024, 0, "ln")
+    iota(T.b0[:], [[5, 2], [10, 64]], 0, 0, "b0")
+    exchange("c")
+    exchange("m", "t")
+    exchange("o")
+    dma("s", T.cc[:], T.lndc[:], "lndc ownc", "cc", "ldc")
+    dma("s", T.memr[0:8, :], T.lndm[:, 0:64, :], "lndm ownm", "memr", "ldm")
+    dma("s", T.oo[:], T.lndo[:], "lndo owno", "oo", "ldo")
+    dma("s", T.th8[0:8, :], T.lndt[:, 0:4, :], "lndt ownm", "th8", "ldt")
+
+    pf = [T.pf[:, k:k + 1] for k in range(16)]
+    fill(T.keep[:], 1.0, "", "keep0")
+    fill(T.vt[:, 1024:4104:1024], -3000.0, "", "vt")
+    fill(T.keep[:, 0:128:16], 0.0, "keep0", "keep")
+    fill(T.c2k[:], 2048.0, "", "c2k")
+    for k, c in ((10, 5120.0), (11, 1024.0), (12, 0.5), (13, -4096.0)):
+        fill(pf[k], c, "", "pf%d" % k)
+    for n in range(8):
+        fill(T.cst[:, 64 * n:64 * n + 64], 77.0 * (n // 2) + 341.0 * (n % 2) + (488.0 if n > 1 else 0.0), "", "cst%d" % n)
+    t1(T.pi[:, 0:1], T.i1[:, 0:1], -128.0, A.add, "i1", "pi0")
+    cp(pf[7], T.i1[:, 0:1], "i1", "pf7")
+    ts(T.li[:], T.i1[:], -1.0, pf[7], A.mult, A.add, "i1 pf7", "li", 128)
+    t1(T.j2[:], T.li[:], 4, A.arith_shift_right, "li", "j2", 128)
+    t1(T.pi[:, 1:2], T.pi[:, 0:1], 4, A.arith_shift_right, "pi0", "pi1")
+    t1(T.pi[:, 2:3], T.pi[:, 0:1], 15, A.bitwise_and, "pi0", "pi2")
+    t1(T.i1m[:], T.i1[:], 15, A.bitwise_and, "i1", "i1m", 128)
+    t1(T.idn[:], T.i1[:], 128.0, A.is_equal, "i1", "idn", 128)
+    cp(T.pf[:, 0:3], T.pi[:, 0:3], "pi0 pi1 pi2", "pf")
+    t1(T.am[:], T.i1m[:], 0.0, A.is_equal, "i1m", "am", 128)
+    t1(T.mr[:], T.li[:, 0:8], pf[1], A.is_equal, "li pf", "mr")
+    t1(pf[4], pf[1], 128.0, A.mult, "pf", "pf4")
+    t1(pf[9], pf[1], 4.0, A.mult, "pf", "pf9")
+    ts(pf[6], pf[2], -100.0, pf[9], A.mult, A.add, "pf pf9", "pf6")
+    t1(T.g8[0:8, :], T.j2[0:8, :], T.pf[0:8, 0:1], A.is_equal, "j2 pf", "g8", 128)
     for r in range(8):
-        t1(T.sel[:, 128 * r:128 * r + 128], T.am[:], T.mr[:, r:r + 1], A.mult, "am mr", "sel%d" % r, 64)
+        act(T.sel[:, 128 * r:128 * r + 128], T.am[:], "am mr", "sel%d" % r, 128, T.mr[:, r:r + 1])
+    fn(T.mneg[:], T.am[:], AF.Identity, pf[13], 4096.0, "am pf13", "mneg", 128)
+    t1(T.yi[:], T.b0[:], pf[4], A.add, "b0 pf4", "yi", 128)
+    tt(T.yc[:], T.yi[:], T.mneg[:], A.add, "yi mneg", "yc", 256)
+    t1(T.lanec[:], T.ln[:], pf[4], A.add, "ln pf4", "lanec", 128)
+    t1(T.blk[:], T.j2[:], pf[1], A.is_equal, "j2 pf", "blk", 128)
+    act(T.b61[:], T.blk[:], "blk", "b61", 128, 30.5)
+    for name, c in (("idq", 2.0 ** -13), ("ndq", -2.0 ** -13), ("nid", -1.0), ("idh", 0.5), ("id9", 2.0 ** -9)):
+        act(T[name][:], T.idn[:], "idn", name, 128, c)
     for t in range(4):
-        t1(T.b0f[:, 16 * t + 8:16 * t + 16], T.b0[:, 8 * t:8 * t + 8], T.pf[:, 3:4], A.add, "b0 pf3 b0f", "b0f%d" % t, 8)
-    cp(T.oi[:, 0:8], T.b0f[:, 8:16], "b0f0", "oi0", 8)
-    t1(T.oi[:, 8:16], T.b0f[:, 8:16], 341.0, A.add, "b0f0", "oi1", 8)
-    t1(T.oj[:], T.oi[:], 1023, A.bitwise_and, "oi0 oi1", "oj", 16)
-    cp(T.o16[:], T.oj[:], "oj", "o16", 16)
-    ts(T.lanec[:], T.li[:], T.pf[:, 4:5], 1024.0 - 2048.0, A.add, A.add, "li pf4", "lanec")
-    ts(T.lane3[:], T.li[:], T.pf[:, 4:5], 4096.0, A.add, A.add, "li pf4", "lane3")
-    for k in range(16):
-        cp(T.ex[:, k:2048:16], T.idn[:], "idn", "ex%d" % k, 64)
-    t1(T.blk[:], T.j2[:], T.pf[:, 1:2], A.is_equal, "j2 pf", "blk")
-    t1(T.b61[:, 120:128], T.mr[:], 61.0, A.mult, "mr b61z", "b61", 8)
-    t1(T.nid[:], T.idn[:], -1.0, A.mult, "idn", "nid")
-    t1(T.idk[:], T.idn[:], 8192.0, A.mult, "idn", "idk", 64)
-    cp(T.idb[:], T.idn[:], "idn", "idb", 64)
-    t1(T.amb[:], T.i1m[:], 0.0, A.is_equal, "i1m", "amb")
-    t1(T.mrk[:], T.mr[:], 8192.0, A.mult, "mr", "mrk", 8)
-    for r in range(8):
-        act(T.selk[:, 128 * r:128 * r + 128], T.amb[:], "amb mrk", "selk%d" % r, T.mrk[:, r:r + 1])
-    for a in range(16):
-        act(T.dg[:, a:2048:16], T.b61[:, 120 - 8 * a:248 - 8 * a], "b61", "dg%d" % a)
-    sels, selks, exs, dgs = names("sel", 8), names("selk", 8), names("ex", 16), names("dg", 16)
+        ts(T.lr[:, 32 * t:32 * t + 32], T.li[:, 0:32], -1.0 * t, pf[6], A.add, A.is_equal, "li pf6", "lr%d" % t)
+    sels, ys = names("sel", 8), [T.pb[:, 0:64], T.pb[:, 64:128]]
 
-    def repeat(b, h, name, mats, mname, start, stop):
-        for r in range(4 * h, 4 * h + 4):
-            c = 128 * (r % 4)
-            mmul(T[b][:, c:c + 128], mats[:, 128 * r:128 * r + 128], T[name][:],
-                 start is True or (start == "first" and r % 4 == 0),
-                 stop is True or (stop == "last" and r % 4 == 3), name + mname, b + " ~" + b[:2])
-        join(4)
+    def repeat(tag, b, src, name, start, stop):
+        mmul(tag, b, [(T[b][:, 64 * r:64 * r + 64], T.sel[:, 128 * r:128 * r + 128], src, name + sels) for r in range(8)], start, stop)
 
-    def table(dst, c0, b, name):
-        act(dst[:, c0:c0 + 512], T[b][:], b, name, busy=0.56)
+    def places(t, h):
+        return [(ys[p], T.idn[:], x, "idn yc cst%d" % (2 * t + p)) for p in range(2)
+                for x in (T.yc[:, half(h)], T.cst[:, half(2 * t + p)])]
 
-    t1(T.x16[:], T.cc[:], -2048.0, A.add, "cc", "x16")
-    repeat("pv0", 0, "x16", T.sel, sels, True, True)
-    repeat("pv1", 1, "x16", T.sel, sels, True, True)
-    table(T.vt, 0, "pv0", "vt0_0")
-    table(T.vt, 512, "pv1", "vt0_1")
-    ts(T.ta[:], T.oo[:], 0.0, -6048.0, A.is_equal, A.mult, "oo", "ta")
-    ts(T.tb[:], T.oo[:], -1.0, 2048.0, A.mult, A.add, "oo", "tb")
-    cp(T.memf[0:8, 0:128], T.memr[0:8, :], "memr", "memf0")
-    tt(T.z16[:], T.ta[:], T.tb[:], A.add, "ta tb", "z16", 256)
-    mmul(T.px[:, 0:128], T.g8[0:8, :], T.memf[0:8, 0:128], True, True, "g8 memf0", "px")
-    repeat("pk0", 0, "z16", T.sel, sels, True, True)
-    repeat("pk1", 1, "z16", T.sel, sels, True, True)
-    table(T.kt, 0, "pk0", "kt0")
-    table(T.kt, 512, "pk1", "kt1")
-    ts(T.tq[:], T.px[:, 0:128], T.pf[:, 2:3], -8192.0, A.not_equal, A.mult, "px pf", "tq")
-    mmul(T.py[:, 0:128], T.idn[:], T.lanec[:], True, False, "idn lanec", "py")
-    mmul(T.py[:, 0:128], T.idn[:], T.tq[:], False, True, "idn tq", "py")
-    cp(T.memf[0:8, 128:136], T.th8[0:8, :], "th8", "memf1", 8)
-    tt(T.xs[:], T.x16[:], T.py[:, 0:128], A.max, "py x16", "xs")
-    ts(T.onep[:], T.tq[:], 0.125, 1024.0, A.mult, A.add, "tq", "onep", 64)
-    mmul(T.px[:, 256:384], T.idn[:], T.onep[:], True, True, "idn onep", "px")
-    mmul(T.px[:, 128:136], T.g8[0:8, :], T.memf[0:8, 128:136], True, True, "g8 memf1", "px", 64)
-    cp(T.thc[:, 0:1], T.px[:, 128 + me:129 + me], "px", "thc0", 1)
-    t1(T.onen[:], T.onep[:], -1.0, A.mult, "onep", "onen", 64)
-    tt(T.t3[:], T.tq[:], T.lanec[:], A.subtract, "tq lanec", "t3", 256)
-    t1(T.zb[:], T.t3[:], -4000.0, A.max, "t3", "zb")
-    t1(T.thc[:, 1:2], T.thc[:, 0:1], 61.0, A.mult, "thc0", "thc1", 1)
-    t1(T.t4[:], T.onep[:], 8.0, A.mult, "onep", "t4")
-    tt(T.oe3[:], T.t4[:], T.lane3[:], A.min, "t4 lane3", "oe3", 256)
+    def lists(h):
+        s, l = str(h), half(h, 0, 8)
+        op("v", lambda: V.tensor_tensor_scan(T.sc[:], T.keep[:], T.pb[:, 0:128], 0.0, A.mult, A.max), "keep pb", "sc", cost(128),
+           tag="sc" + s)
+        t1(T.oj[:, l], T.sc[:, 15:128:16], 1023, A.bitwise_and, "sc", "oj" + s)
+        cp(T.o16[:, l], T.oj[:, l], "oj" + s, "o16" + s)
 
-    ends = [0, 24, 56, 88, 112, 128]
-    sums = {1: (0, 56), 3: (56, 112)}
-    share = 8
-    vts = " vt0"
-    for t in range(4):
-        last = t == 3
-        B = 1024 * (t + 1)
-        new = " vt%d_0 vt%d_1" % (t, t)
-        vts += new
-        xn = "xf" if last else "x16"
-        x = T[xn]
-        win = T.vt[:, B - 1024:B]
-        low = T.py[:, 384:512]
-        tt(T.x1[:], win.indirect(T.o16[:, 0:8]), T.xs[:], A.max, "o16 xs" + new, "x1", 220)
-        tt(x[:], win.indirect(T.o16[:, 8:16]), T.x1[:], A.max, "o16 x1" + new, xn, 220)
-        ts(T.off[:], x[:], B - 2048.0, 2048.0, A.min, A.add, xn, "off", 128 if last else 64)
-        for c in range(5):
-            lo, hi = ends[c], ends[c + 1]
-            if c == 3:
-                cp(T.gb[:, 16 * lo:16 * (lo + share)], T.vt[:, 0:B + 1].indirect(T.off[:, lo:lo + share]), "off" + vts, "gd",
-                   20 + 25 * share)
-                lo += share
-            act(T.gb[:, 16 * lo:16 * hi], T.vt[:, 0:B + 1].indirect(T.off[:, lo:hi]), "off" + vts, "gb%d ~gb" % c,
-                busy=0.06 + 0.025 * (hi - lo))
-        own = "z16" if t == 0 else "ownk"
-        tt(T.k1[:], T.kt[:].indirect(T.o16[:, 0:8]), T[own][:], A.max, "kt0 kt1 o16 " + own, "k1", 220)
-        tt(T.k2[:], T.kt[:].indirect(T.o16[:, 8:16]), T.k1[:], A.max, "kt0 kt1 o16 k1", "k2", 220)
-        ts(T.t8[:], T.k2[:], MAGIC, -MAGIC, A.add, A.add, "k2", "t8")
-        mmul(T.py[:, 0:128], T.k2[:], T.nid[:], True, False, "k2 nid", "py", 512)
-        mmul(T.py[:, 0:128], T.t8[:], T.idn[:], False, True, "t8 idn", "py")
-        cp(T.lowt[:], T.py[:, 0:128], "py", "lowt")
-        mmul(low, T.lowt[:], T.idn[:], True, True, "lowt idn", "py")
+    for h in both:
+        mmul("y", "pb", places(0, h))
+        lists(h)
+
+    now[0] = -1
+    for h in both:
+        s, b = str(h), ("pb", "pa")[h]
+        t1(T.x16[:, half(h)], T.cc[:, h:128:2], -2048.0, A.add, "cc", "x16" + s)
+        repeat("vt" + s, b, T.x16[:, half(h)], "x16" + s, "each", True)
+        act(T.vt[:, h:1024:2], T[b][:], b, "vt%d@0" % h, 512)
+    cp(T.memf[0:8, 0:128], T.memr[0:8, :], "memr", "memf", 128)
+    mmul("mem", "pc0", [(T.pc0[:, half(h)], T.g8[0:8, :], T.memf[0:8, h:128:2], "g8 memf") for h in both], "each")
+    ts(T.tq[:], T.pc0[:, 0:128], pf[2], -8192.0, A.not_equal, A.mult, "pc0 pf", "tq", 128)
+    mmul("e", "pc1", [(T.pc1[:, 0:128], T.idn[:], T.lanec[:], "idn lanec"), (T.pc1[:, 0:128], T.idn[:], T.tq[:], "tq")], n=128)
+    tt(T.xs[:], T.x16[:], T.pc1[:, 0:128], A.max, "pc1 x160 x161", "xs0 xs1", 128)
+    t1(T.om16[:], T.oo[:], -2048.0, A.add, "oo", "om16", 128)
+    ts(T.pe0[:, 0:128], T.oo[:], -6048.0, 4000.0, A.mult, A.add, "oo", "pe0", 128)
+    tt(T.low0[:], T.om16[:], T.pe0[:, 0:128], A.max, "om16 pe0", "low0", 128)
+    for h in both:
+        b = "pk%d" % h
+        repeat("kt%d" % h, b, T.low0[:, h:128:2], "low0", "each", True)
+        cp(T.kt[:, h:1024:2], T[b][:], b, "kt%d@0" % h, 512)
+    for h in both:
+        fn(T["pc%d" % h][:, 320:384], T.pc1[:, half(h)], AF.Relu, pf[10], 1.0, "pc1 pf10", "pc%d" % h, tag="e%d" % h)
+    fn(T.onep[:], T.tq[:], AF.Relu, pf[11], 0.125, "tq pf11", "onep", 128)
+    cp(T.memf[0:8, 128:136], T.th8[0:8, :], "th8", "thf")
+    mmul("th", "pa", [(T.pa[:, 0:8], T.g8[0:8, :], T.memf[0:8, 128:136], "g8 thf")])
+    thc = [T.thc[:, k:k + 1] for k in range(3)]
+    for k, (scale, bias) in enumerate(((-1.0, 0.5), (-1.0, 2.5), (2.0, -16.0))):
+        ts(thc[k], T.pa[:, me:me + 1], scale, bias, A.mult, A.add, "pa", "thc%d" % k)
+    mmul("zb", "pa", [(T.pa[:, 0:128], T.idn[:], T.tq[:], "idn tq"), (T.pa[:, 0:128], T.nid[:], T.lanec[:], "nid lanec")], n=128)
+    t1(T.zb[:], T.pa[:, 0:128], -4000.0, A.max, "pa", "zb", 128)
+    for h in both:
+        b = "pc%d" % h
+        mmul("one%d" % h, b, [(T[b][:, 256:320], T.idn[:], T.onep[:, half(h)], "idn onep")])
+
+    def front(t, h, vts):
+        s, c, B, last = str(h), half(h), 1024 * (t + 1), t == 3
+        new = " o16%s vt0@%d vt1@%d" % (s, t, t)
+        xn = ("xf" if last else "x16") + s
+        x, win, at = T[xn[:-1]][:, c], T.vt[:, B - 1024:B], 1024 * h
+        tt(T.x1[:, c], win.indirect(T.o16[:, 8 * h:8 * h + 4]), T.xs[:, c], A.max, "xs" + s + new, "x1" + s, 120)
+        tt(x, win.indirect(T.o16[:, 8 * h + 4:8 * h + 8]), T.x1[:, c], A.max, "x1" + s + new, xn, 120)
+        ts(T.off[:, c], x, B - 2048.0, 2048.0, A.min, A.add, xn, "off" + s)
+        for n, (lo, hi) in enumerate(PIECES):
+            act(T.gb[:, at + 16 * lo:at + 16 * hi], T.vt[:, 0:B + 1].indirect(T.off[:, 64 * h + lo:64 * h + hi]),
+                "off" + s + vts, "g%s%s" % ("ab"[n], s), 15 + 25 * (hi - lo))
         if last:
-            t1(T.xo[:], T.xf[:], 2048.0, A.add, "xf", "xo")
-            dma("s", T.stgx[:], T.xo[:], "xo", "stgx ~s0", "dx")
-            dma("s", T.lndx[me], T.xo[mine, :], "xo", "ownx ~s0", "dxo")
-            exchange(lambda r: T.stgx[r], T.lndx[me], "stgx", "arrx", "lndx")
-            t1(T.t2[:], low, 3500.0, A.is_lt, "py", "t2")
-            t1(T.pv0[:, 0:128], low, 2048.0, A.add, "py", "pv0")
-            tt(T.pv1[:, 0:128], T.t2[:], T.pv0[:, 0:128], A.mult, "t2 pv0", "pv1")
-            tt(T.py[:, 128:256], T.oe3[:], T.pv1[:, 0:128], A.subtract, "oe3 pv1", "py")
+            t1(T.xo[:, h:128:2], x, 2048.0, A.add, xn, "xo" + s)
+            return
+        repeat("vt" + s, "pa", x, xn, "each", True)
+        act(T.vt[:, B + h:B + 1024:2], T.pa[:], "pa", "vt%d@%d" % (h, t + 1) + (vts if h == 0 else ""), 512)
+
+    def keys(t, h):
+        s, c = str(h), half(h)
+        pe, pk, low = "pe" + s, "pk" + s, T.low[:, c]
+        t8, tn = T.t8[:, half(h, 128 * t)], "t8%d@%d" % (h, t)
+        win, kn = T.kt[:, half(t % 2, 0, 1024)], " o16%s kt0@%d kt1@%d" % (s, t % 2, t % 2)
+        one, two = win.indirect(T.o16[:, 8 * h:8 * h + 4]), win.indirect(T.o16[:, 8 * h + 4:8 * h + 8])
+        if t == 0:
+            tt(T.k1[:, c], one, T.low0[:, h:128:2], A.min, "low0" + kn, "k1" + s, 120)
+            tt(low, two, T.k1[:, c], A.min, "k1" + s + kn, "k2%s low%s" % (s, s), 120)
         else:
-            repeat("pv0", 0, "x16", T.sel, sels, True, True)
-            repeat("pv1", 1, "x16", T.sel, sels, True, True)
-            t1(T.ft[:, 128:256], T.t8[:], 21.0 / 8192.0, A.mult, "t8", "ft1", 64)
-            tt(T.xs[:], T.x16[:], T.px[:, 256:384], A.add, "x16 px", "xs")
-            repeat("pk0", 0, "t8", T.sel, sels, "first", False)
-            repeat("pk1", 1, "t8", T.sel, sels, "first", False)
-            for n, name in enumerate(["zb"] + ["onen"] * t):
-                mmul(T.py[:, 128:256], T.idn[:], T[name][:], n == 0, False, "idn " + name, "py")
-            mmul(T.py[:, 128:256], T.lowt[:], T.idn[:], False, True, "lowt idn", "py")
-        tt(T.sf[:], x[:], low, A.is_ge, xn + " py", "sf")
-        for c in range(5):
-            lo, hi = ends[c], ends[c + 1]
-            b = "pe%d" % (c % 2)
-            w = 16 * (hi - lo)
-            mmul(T[b][:, 0:w], T.lowt[:], T.ex[:, 16 * lo:16 * hi], True, True, "lowt" + exs, b + " ~ex", w)
-            tt(T.f1[:, 16 * lo:16 * hi], T.gb[:, 16 * lo:16 * hi], T[b][:, 0:w], A.is_ge,
-               "gb%d %s" % (c, b) + (" gd" if c == 3 else ""), "f1_%d ~f1" % c, w)
-            if c in sums:
-                l0, l1 = sums[c]
-                if c == 3:
-                    mmul(T.px[:, 0:l0], T.idb[:], T.sf[:, 0:l0], False, False, "idb sf", "px", l0)
-                    mmul(T.px[:, l0:128], T.idb[:], T.sf[:, l0:128], False, False, "idb sf", "px", 128 - l0)
-                for k in range(16):
-                    mmul(T.px[:, l0:l1], T.idb[:], T.f1[:, 16 * l0 + k:16 * l1:16], c == 1 and k == 0, False,
-                         "idb f1_%d f1_%d" % (c - 1, c), "px", 64)
-                    if k % 4 == 3:
-                        join(4)
-        op("v", lambda: V.tensor_tensor_scan(T.sc[:], T.keep[:], T.f1[:, 1792:2048], 0.0, A.mult, A.add), "keep f1_4", "sc")
-        mmul(T.px[:, 112:128], T.idb[:], T.sc[:, 15:256:16], False, True, "idb sc", "px", 64)
+            tt(T.k1[:, c], one, T.ownk[:, c], A.max, "ownk" + s + kn, "k1" + s, 120)
+            tt(T.k2[:, c], two, T.k1[:, c], A.max, "k1" + s + kn, "k2" + s, 120)
+            ts(t8, T.k2[:, c], MAGIC, -MAGIC, A.add, A.add, "k2" + s, tn)
+            tt(low, t8, T.k2[:, c], A.subtract, tn + " k2" + s, "low" + s, 128)
+        mmul("low" + s, pe, [(T[pe][:, k:256:4], T.idn[:], low, "idn low" + s) for k in range(4)], "each")
+        if t == 3:
+            ts(T.t2[:, c], low, 3500.0, -6048.0, A.is_ge, A.mult, "low" + s, "t2" + s)
+            mmul("mark" + s, pk, [(T[pk][:, 0:64], T.idn[:], x, "idn c2k low%s t2%s" % (s, s)) for x in (T.c2k[:, c], low, T.t2[:, c])],
+                 True, False)
+            return
         if t > 0:
-            act(T.rh[:, 128 * t - 128:128 * t], T.py[:, 256:384], "py", "rh%d" % (t - 1), 1.0 / 8192.0)
-        if not last:
-            table(T.vt, B, "pv0", "vt%d_0" % (t + 1) + vts)
-            table(T.vt, B + 512, "pv1", "vt%d_1" % (t + 1))
-        t1(T.ft[:, 0:128], T.px[:, 0:128], T.thc[:, 0:1], A.is_ge, "px thc0", "ft0")
-        mmul(T.py[:, 0:128], T.blk[:], T.ft[:, 0:128], True, True, "blk ft0", "py")
-        if not last:
-            mmul(T.px[:, 0:16], T.idn[:], T.b0f[:, 16 * (t + 1):16 * (t + 2)], True, False, "idn b0f%d" % (t + 1), "px", 64)
-            for a in range(16):
-                mmul(T.px[:, 0:16], T.dg[:, 128 * a:128 * a + 128], T.ft[:, a:256:16], False, a == 15, "ft0 ft1" + dgs, "px", 64)
-            join(16)
-        t1(T.up[:], T.py[:, 0:128], T.thc[:, 0:1], A.is_ge, "py thc0", "up")
-        tt(T.mm[:], T.py[:, 128:256], T.up[:], A.mult, "py up", "mm")
-        if last:
-            mmul(T.pe1[:, 0:128], T.idn[:], T.t8[:], True, False, "idn t8", "pe1")
-            mmul(T.pe1[:, 0:128], T.idk[:], T.up[:], False, True, "idk up", "pe1")
-            act(T.rh[:, 384:512], T.pe1[:, 0:128], "pe1", "rh3", 1.0 / 8192.0)
-            tt(T.wo[:], T.mm[:], T.pv1[:, 0:128], A.add, "mm pv1", "wo")
-            break
-        tt(T.z16[:], T.mm[:], low, A.subtract, "mm py", "z16")
-        for h, b in enumerate(("pk0", "pk1")):
-            repeat(b, h, "up", T.selk, selks, False, False)
-            repeat(b, h, "z16", T.sel, sels, False, "last")
-            table(T.kt, 512 * h, b, "kt%d" % h)
-        mmul(T.py[:, 256:384], T.idn[:], T.t8[:], True, False, "idn t8", "py")
-        mmul(T.py[:, 256:384], T.idk[:], T.up[:], False, True, "idk up", "py")
-        tt(T.ownk[:], T.z16[:], T.py[:, 256:384], A.add, "z16 py", "ownk")
-        ts(T.tu[:], T.px[:, 0:8], T.thc[:, 1:2], 16.0, A.is_ge, A.mult, "px thc1", "tu", 8)
-        tt(T.tv[:], T.px[:, 0:8], T.tu[:], A.add, "px tu", "tv", 8)
-        tt(T.oi[:, 0:8], T.px[:, 8:16], T.tv[:], A.add, "px tv", "oi0", 8)
-        t1(T.oi[:, 8:16], T.oi[:, 0:8], 341.0, A.add, "oi0", "oi1", 8)
-        t1(T.oj[:], T.oi[:], 1023, A.bitwise_and, "oi0 oi1", "oj", 16)
-        cp(T.o16[:], T.oj[:], "oj", "o16", 16)
+            repeat("kT" + s, pk, t8, tn, True, False)
 
-    rs = names("rh", 4)
-    dma("s", T.stgw[:], T.wo[:], "wo", "stgw ~s0", "dw")
-    dma("a", T.stgr[:], T.rh[0:128:16, :], rs, "stgr", "dr")
-    dma("s", T.lndw[me], T.wo[mine, :], "wo", "ownw ~s0", "dwo")
-    dma("a", T.lndr[me], T.rh[16 * me:16 * me + 1, :], rs, "ownr", "dro")
-    dma("s", T.yx[:], T.lndx[:], "lndx ownx", "~s0", "dy")
-    exchange(lambda r: T.stgw[r], T.lndw[me], "stgw", "arrw", "lndw")
-    exchange(lambda r: T.stgr[r], T.lndr[me], "stgr", "arrr", "lndr")
-    dma("s", T.yo[:], T.lndw[:], "lndw ownw", "~s0", "dyo")
-    dma("a", T.yr[:], T.lndr[:], "lndr ownr", "", "dyr")
+    def back(t, h):
+        s, c, last = str(h), half(h), t == 3
+        xn = "xf" if last else "x16"
+        t8, tn = T.t8[:, half(h, 128 * t)], "t8%d@%d" % (h, t)
+        up, un = T.up[:, half(h, 128 * t)], "up%d@%d" % (h, t)
+        pe, pk, pc, at = "pe" + s, "pk" + s, "pc" + s, 1024 * h
+        low, cnt, gbs, b = T[pe][:, 0:256:4], T[pc][:, 0:64], " ga%s gb%s" % (s, s), ("pb", "pa")[h]
+        for k in range(4):
+            f, m, name = at + 256 * k, "idn", "f%s%s" % ("abcd"[k], s)
+            if k == 2:
+                tt(T.sf[:, c], T[xn][:, c], low, A.is_ge, xn + s + " " + pe, "sf" + s)
+                mmul("sf" + s, pc, [(cnt, T.idn[:], T.sf[:, c], "idn sf" + s)], False, False)
+            if last and k == 1:
+                m = "idh"
+                mmul("g" + s, b, [(T[b][:, 256:512], T.idn[:], T.gb[:, at + k:at + 1024:4], "idn" + gbs)], True, False, 256)
+                mmul("gl" + s, b, [(T[b][:, 256 + n:512:4], T.nid[:], T.low[:, c], "nid low" + s) for n in range(4)], False, True)
+                fn(T.f1[:, f:f + 256], T[b][:, 256:512], AF.Sign, pf[12], 1.0, b + " pf12", name, 256)
+            else:
+                tt(T.f1[:, f:f + 256], T.gb[:, at + k:at + 1024:4], T[pe][:, 0:256], A.is_ge, pe + gbs, name, 256)
+            mmul(name, pc, [(cnt, T[m][:], T.f1[:, f + n:f + 256:4], m + " " + name) for n in range(4)], k == 0, k == 3)
+        if not last:
+            d = T[pe][:, 320:384]
+            mmul("d" + s, pe, [(d, T.idq[:], T.zb[:, c], "idq zb")] + [(d, T.ndq[:], T.onep[:, c], "ndq onep")] * t +
+                 [(d, T.idq[:], T.low[:, c], "low" + s)])
+        fn(T.ft[:, c], cnt, AF.Sign, thc[1 if last else 0], 1.0, pc + " thc0 thc1", "ft" + s)
+        mmul("S" + s, pc, [(T[pc][:, 64:128], T.blk[:], T.ft[:, c], "blk ft" + s)])
+        if not last:
+            mmul("y" + s, "pb", places(t + 1, h) + [(y, T.id9[:], t8, "id9 " + tn) for y in ys if t > 0], True, False)
+            mmul("yS" + s, "pb", [(y, T.b61[:], T.ft[:, c], "b61 ft" + s) for y in ys], False, False)
+        ts(up, T[pc][:, 64:128], thc[2], 8192.0, A.is_ge, A.mult, pc + " thc2", un)
+        if last:
+            mmul("mup" + s, pk, [(T[pk][:, 0:64], T.nid[:], up, "nid " + un)], False, True)
+            tt(T.mm[:, c], T[pc][:, 320:384], up, A.min, pc + " " + un, "mm" + s)
+            tt(T.wo[:, h:128:2], T.mm[:, c], T[pk][:, 0:64], A.max, "mm%s %s" % (s, pk), "wo" + s)
+            r = T[b][0:32, 0:64]
+            terms = [(r, T.lr[:, 32 * u:32 * u + 32], T[src][:, half(h, 128 * u)], "lr%d %s%d@%d" % (u, src, h, u))
+                     for u, src in ((0, "up"), (1, "t8"), (1, "up"), (2, "t8"), (2, "up"), (3, "t8"), (3, "up"))]
+            mmul("R" + s, b, terms[:6], True, False)
+            mmul("Rup" + s, b, terms[6:], False, True)
+            act(T.rc[0:32, h:128:2], r, b, "rc" + s, scale=2.0 ** -13)
+            return
+        mmul("yup" + s, "pb", [(y, T.id9[:], up, "id9 " + un) for y in ys], False, True)
+        tt(T.mm[:, c], T[pe][:, 320:384], up, A.mult, pe + " " + un, "mm" + s)
+        tt(T.z16[:, c], T.mm[:, c], low, A.subtract, "mm%s %s" % (s, pe), "z16" + s)
+        repeat("kup" + s, pk, up, un, t == 0, False)
+        repeat("kz" + s, pk, T.z16[:, c], "z16" + s, False, True)
+        n = (t + 1) % 2
+        act(T.kt[:, 1024 * n + h:1024 * n + 1024:2], T[pk][:], pk, "kt%d@%d" % (h, n), 512)
+        o = T[pc][:, 128:192]
+        mmul("own" + s, pc, [(o, T.idn[:], up, "idn " + un)] + [(o, T.idn[:], t8, tn)] * (t > 0))
+        tt(T.ownk[:, c], T.z16[:, c], o, A.add, pc + " z16" + s, "ownk" + s)
+        tt(T.xs[:, c], T.x16[:, c], T[pc][:, 256:320], A.add, pc + " x16" + s, "xs" + s)
+        lists(h)
+
+    vts = " vt"
+    for t in range(4):
+        now[0] = t
+        vts += " vt0@%d vt1@%d" % (t, t)
+        for h in both:
+            front(t, h, vts)
+        if t == 3:
+            dma("s", T.stgx[:], T.xo[:], "xo0 xo1", "stgx", "putx")
+            dma("s", T.lndx[me], T.xo[mine, :], "xo0 xo1", "ownx", "ownx")
+            exchange("x")
+        for h in both:
+            keys(t, h)
+        for h in both:
+            back(t, h)
+
+    dma("s", T.stgw[:], T.wo[:], "wo0 wo1", "stgw", "putw")
+    dma("a", T.stgr[:], T.rc[0:32, :], "rc0 rc1", "stgr", "putr")
+    dma("s", T.lndw[me], T.wo[mine, :], "wo0 wo1", "ownw", "ownw")
+    dma("a", T.lndr[me], T.rc[4 * me:4 * me + 4, :], "rc0 rc1", "ownr", "ownr")
+    dma("s", T.yx[:], T.lndx[:], "lndx ownx", "yx", "ldx")
+    exchange("r")
+    exchange("w")
+    dma("s", T.yo[:], T.lndw[:], "lndw ownw", "yo", "ldw")
+    dma("a", T.yr[:], T.lndr[:], "lndr ownr", "yr", "ldr")
     emit(ops, g, T, arrivals)

from concourse.bass import DstId, RemoteDMATransfer
from concourse.mybir import AluOpType as A
from concourse.mybir import ActivationFunctionType as AF

H, F, I, U = "float16", "float32", "int32", "uint16"
PSUM = ("pa", "pb", "pk0", "pk1", "pe0", "pe1", "pc0", "pc1")
SCRATCH = {"stgt": ("dram", [128, 2], I), "lndt": ("dram", [8, 128, 2], I)}
for _n, _w, _dt in (("c", 16, I), ("m", 2, I), ("o", 16, I), ("x", 16, F), ("w", 16, F), ("r", 4, F)):
    SCRATCH["stg" + _n] = ("dram", [8, 128, _w], _dt)
    SCRATCH["lnd" + _n] = ("dram", [8, 128, _w], _dt)
for _dt, _w, _names in (
        (I, 128, "i1 i1m j2 li ln b0 cc oo memr sc"), (I, 8, "pi th8"), (I, 16, "oj"),
        (U, 128, "off"), (U, 16, "o16"),
        (F, 8, "mr thc"), (F, 16, "pf"), (F, 128, "xf xs x1 xo k1 k2 ownk mm wo rc yi"), (F, 2048, "kt"), (F, 4104, "vt"),
        (H, 128, "c2k idn idq ndq nid idh id9 am blk b61 g8 mneg lanec x16 om16 low0 low z16 tq onep zb sf ft t2 yc y0 keep"),
        (H, 128, "lr"), (H, 136, "memf"), (H, 512, "t8 up cst"), (H, 1024, "sel"), (H, 2048, "f1 gb")):
    for _n in _names.split():
        SCRATCH[_n] = ("sbuf", [128, _w], _dt)
for _n in PSUM:
    SCRATCH[_n] = ("psum", [128, 512], F)
SEMAPHORES = ["g", "v", "a", "p", "sent", "arrt", "ldt"] + [a + b for a in ("put", "own", "arr", "ld") for b in "cmoxwr"]
MAGIC = 1.5 * 2.0 ** 36
PIECES = ((0, 32), (32, 64))

ORDER = """
s.e1< l.x11< mm0> *kz1> s.*mem< oj1> s.onep l.off0 l.*mark1 x11 kt0> l.ga1 ga1 l.fb0 s.kt0 x10 x161 *fb0> s.*one0 fd0>
s.*one1 l.fa0 l.k21 s.kt1 *y0> o161> *kz0> l.off1 l.sf0< *S0> ownk1> *d0> s.*kt0 t80 l.*fd0 x160 s.xs0< l.*S0 s.*zb
ft1 *yS0> *kT1 l.*g1 k11 up0 *own0> l.*fd1 oj0 l.*gl1 *fd0 l.xo0 *kup0> off0 s.thc2 *vt1 s.*vt1< l.gb1 k21 s.x161<
l.k20 k10 l.t81 gb1 s.thc0 ga0 s.thc1 s.memf< gb0 l.fb1 vt1 t81 l.t80 k20 s.e0< l.gb0 l.ga0 l.low1 sf1 s.x160< s.vt1<
l.low0 low0 fa1 l.t21 s.zb l.k11< l.fc0 l.xo1 l.*low1< l.t20 l.rc1< l.fa1 *fd1 l.fd1 l.sf1 up1 l.*fc1 *fb1 off1< fb1
l.fc1 l.*low0 o160 *sf1< *fa0 *d1 s.*kt1< *low0< z160 l.*fc0 fc1 fd1 xs1 sc1 l.*sf0 s.*vt0< sc0 *kT0< l.ft1 l.rc0 *sf0
fa0 l.*gl0 z161 *fa1< fc0 fb0 l.*fa1 ft0 s.vt0< vt0 kt1< *S1 sf0 l.*g0 l.xf0< *yup1 *low1< l.*mark0< mm1 s.tq< s.thf<
s.pe0< l.*fb0 l.k10< *vt0 xs0< l.*sf1 l.*fb1 *fc1< l.up0 s.om16< l.fd0 s.*e< s.*th< l.*Rup0 *y1< *fc0 l.xf1< l.*fa0
*yS1 ownk0 l.x10< l.*S1 *own1 *kup1 *yup0 l.*R1 low1< s.low0< l.up1 l.ft0 l.*Rup1 l.mm1 l.*R0 l.*mup1 l.mm0 l.*mup0
l.wo1 l.wo0
"""


def needs(ops):
    writer, readers, deps, follow, lines = {}, {}, [], [], {}
    for k, (q, fn, rd, wr, sem, busy, lat, t, tag) in enumerate(ops):
        d = set()
        for r in rd:
            d.update(writer.get(r, []))
            if r in PSUM:
                d.update(x for x in readers.get(r, []) if ops[x][0] != q)
        for w in wr:
            d.update(writer.get(w, []))
            d.update(readers.get(w, []))
        f = set()
        if q == "p":
            f = set(x for x in d if ops[x][0] == "p")
            d -= f
        if sem is not None and fn is not None:
            f.update(lines.get(q, []))
            lines[q] = [k]
        for r in rd:
            readers.setdefault(r, []).append(k)
        for w in wr:
            same = sem is not None and w in writer and all(ops[x][4] == sem for x in writer[w]) and not readers.get(w)
            if same:
                d -= set(writer[w])
                writer[w] = writer[w] + [k]
            else:
                writer[w] = [k]
            readers[w] = []
        d.discard(k)
        deps.append(d)
        follow.append(f)
    return deps, follow


def arrange(ops, deps, follow):
    place = {name.strip("<>"): (name.count(">") - name.count("<"), n) for n, name in enumerate(ORDER.split())}
    key = [(max(o[7], 0) + place[o[8]][0], place[o[8]][1]) if o[8] in place else (-9, k) for k, o in enumerate(ops)]
    done, order, left = set(), [], sorted(range(len(ops)), key=lambda k: key[k])
    while left:
        k = next(k for k in left if (deps[k] | follow[k]) <= done)
        left.remove(k)
        done.add(k)
        order.append(k)
    return order


def emit(ops, g, T, arrivals):
    queues = {"g": g, "v": g.vector, "a": g.scalar, "p": g.tensor, "s": g.sync}
    deps, follow = needs(ops)
    order = arrange(ops, deps, follow)
    pos, count = {}, {}
    for k in order:
        src = ops[k][4] if ops[k][4] is not None else ops[k][0]
        count[src] = count.get(src, 0) + 1
        pos[k] = (src, count[src])
    known = {q: {} for q in queues}
    after, waits, needed = {}, {}, set()
    for k in order:
        q = ops[k][0]
        want = {}
        for x in deps[k]:
            src, c = pos[x]
            if ops[x][1] is not None and ops[x][4] in arrivals:
                continue
            if ops[x][4] is not None:
                c = count[src]
            if c > want.get(src, (0, 0))[0]:
                want[src] = (c, x)
        lst = []
        if ops[k][1] is not None:
            for src, (c, x) in sorted(want.items(), key=lambda it: -len(after[it[1][1]])):
                if known[q].get(src, 0) >= c:
                    continue
                lst.append((src, x))
                needed.add(x)
                known[q][src] = c
                for s2, c2 in after[x].items():
                    if known[q].get(s2, 0) < c2:
                        known[q][s2] = c2
        waits[k] = lst
        after[k] = dict(known[q]) if ops[k][1] is not None else {}
    val, total = {}, {}
    for k in order:
        if ops[k][4] is None and k in needed:
            total[ops[k][0]] = total.get(ops[k][0], 0) + 1
            val[k] = total[ops[k][0]]
    for src in count:
        if src in arrivals:
            total[src] = arrivals[src]
        elif src not in queues:
            total[src] = 16 * count[src]
    waited = {}
    for k in order:
        q, fn, rd, wr, sem = ops[k][:5]
        for src, x in waits[k]:
            c = val[x] if ops[x][4] is None else total[src]
            queues[q].wait_ge(T.sem[src], c)
            waited[src] = max(waited.get(src, 0), c)
        if fn is None:
            continue
        ins = fn()
        if sem is None:
            if k in needed:
                ins.then_inc(T.sem[q], 1)
        elif sem not in arrivals:
            ins.then_inc(T.sem[sem], 16)
    for src in sorted(total):
        if waited.get(src, 0) < total[src]:
            g.wait_ge(T.sem[src], total[src])


def rank_program(g, core, T, topo):
    me = T.rank_of(core)
    if me is None:
        return
    cores = list(T.cores)
    others = [r for r in range(8) if r != me]
    V, S, P = g.vector, g.scalar, g.tensor
    ops, now = [], [-2]

    def op(q, fn, rd, wr, busy, sem=None, lat=None, tag=None):
        tag = {-2: "c.", -1: "s.", 3: "l."}.get(now[0], "") + (tag or wr.split()[0].split("@")[0])
        ops.append((q, fn, rd.split(), wr.split(), sem, busy, busy if lat is None else lat, now[0], tag))

    def cost(n):
        return 0.03 + 0.001 * max(64, n)

    def ts(out, in0, s1, s2, op0, op1, rd, wr, n=64):
        op("v", lambda: V.tensor_scalar(out, in0, s1, s2, op0, op1), rd, wr, cost(n))

    def t1(out, in0, s1, op0, rd, wr, n=64):
        op("v", lambda: V.tensor_scalar(out, in0, s1, None, op0), rd, wr, cost(n))

    def tt(out, in0, in1, o, rd, wr, n=64):
        op("v", lambda: V.tensor_tensor(out, in0, in1, o), rd, wr, cost(n))

    def cp(out, in_, rd, wr, n=64):
        op("v", lambda: V.tensor_copy(out, in_), rd, wr, cost(n))

    def fill(out, c, rd, wr, n=64):
        op("v", lambda: V.memset(out, c), rd, wr, cost(n))

    def act(out, in_, rd, wr, n=64, scale=1.0):
        op("a", lambda: S.activation(out, in_, AF.Copy, scale=scale), rd, wr, 0.02 + cost(n))

    def fn(out, in_, f, bias, scale, rd, wr, n=64, tag=None):
        op("a", lambda: S.activation(out, in_, f, bias=bias, scale=scale), rd, wr, 0.02 + cost(n), tag=tag)

    def mmul(tag, b, terms, start=True, stop=True, n=64):
        def run():
            for k, x in enumerate(terms):
                each = start == "each"
                ins = P.matmul(x[0], x[1], x[2], each or (start and k == 0), each or (stop and k == len(terms) - 1))
            return ins
        op("p", run, " ".join(x[3] for x in terms), b, 0.0005 * max(64, n) * len(terms), tag="*" + tag)

    def dma(q, out, in_, rd, wr, sem):
        eng = g.sync if q == "s" else g.scalar
        op(q, lambda: eng.dma_start(out, in_), rd, wr, 0.08, sem, 1.9 if sem in ("putr", "ldr", "ldm", "ldt") else 2.3, "dma")

    def iota(out, pattern, base, cm, name):
        op("g", lambda: g.iota(out, pattern, base, cm), "", name, 0.39)

    def names(stem, n):
        return " " + " ".join(stem + str(k) for k in range(n))

    arrivals = {"arr" + x: len(others) for x in "cmotxwr"}
    arrivals["sent"] = 0

    def exchange(x, common=""):
        trs, ids, used, free = [], [], 0, -1
        for r in others:
            rid, pid = topo.addr(cores[r], core)
            ids.append(DstId(rid=rid, pnc=pid))
            e = [n for n in topo.engines(core, cores[r]) if not used >> n & 1][0]
            used |= 1 << e
            free &= topo.mask(core, cores[r])
            trs.append(RemoteDMATransfer(dst_ids=[ids[-1]], dma_engine_mask=1 << e, remote_sem=T.sem["arr" + x],
                                         src=T["stg" + x][r], dst=T["lnd" + x][me]))
        if common:
            free &= ~used
            trs.append(RemoteDMATransfer(dst_ids=ids, dma_engine_mask=free & -free, remote_sem=T.sem["arr" + common],
                                         src=T["stg" + common][:], dsts=[T["lnd" + common][me]] * len(ids)))
        arrivals["sent"] += len(trs)
        op("g", lambda: g.remote_dma_fused(trs, local_sem=T.sem.sent), "stg" + x, "call" + x, 0.5, "sent", 3.5)
        for y in x + common:
            op("n", None, "call" + x, "lnd" + y, 0.0, "arr" + y, 0.001)

    mine = slice(16 * me, 16 * me + 16)
    both = (1, 0)

    def half(h, at=0, w=64):
        return slice(at + w * h, at + w * h + w)

    dma("s", T.stgc[:], T.col[:], "", "stgc", "putc")
    dma("a", T.stgm[:, 0:64, :], T.mem[:], "", "stgm", "putm")
    dma("s", T.stgm[:, 64:128, :], T.mem[:], "", "stgm", "putm")
    dma("a", T.stgt[0:4, :], T.th[:], "", "stgm", "putm")
    dma("s", T.stgt[4:128, :], T.mem[0:2, 0:124], "", "stgm", "putm")
    dma("a", T.stgo[:], T.om[:], "", "stgo", "puto")
    dma("s", T.lndc[me], T.col[mine, :], "", "ownc", "ownc")
    dma("a", T.lndo[me], T.om[mine, :], "", "owno", "owno")
    dma("s", T.lndm[me, 0:64, :], T.mem[me, :], "", "ownm", "ownm")
    dma("a", T.lndt[me, 0:4, :], T.th[:], "", "ownm", "ownm")
    iota(T.i1[:], [[-1, 128]], 128, 1, "i1")
    iota(T.ln[:], [[1, 2], [2, 64]], -1024, 0, "ln")
    iota(T.b0[:], [[5, 2], [10, 64]], 0, 0, "b0")
    exchange("c")
    exchange("m", "t")
    exchange("o")
    dma("s", T.cc[:], T.lndc[:], "lndc ownc", "cc", "ldc")
    dma("s", T.memr[0:8, :], T.lndm[:, 0:64, :], "lndm ownm", "memr", "ldm")
    dma("s", T.oo[:], T.lndo[:], "lndo owno", "oo", "ldo")
    dma("s", T.th8[0:8, :], T.lndt[:, 0:4, :], "lndt ownm", "th8", "ldt")

    pf = [T.pf[:, k:k + 1] for k in range(16)]
    fill(T.keep[:], 1.0, "", "keep0")
    fill(T.vt[:, 1024:4104:1024], -3000.0, "", "vt")
    fill(T.keep[:, 0:128:16], 0.0, "keep0", "keep")
    fill(T.c2k[:], 2048.0, "", "c2k")
    for k, c in ((10, 5120.0), (11, 1024.0), (12, 0.5), (13, -4096.0)):
        fill(pf[k], c, "", "pf%d" % k)
    for n in range(8):
        fill(T.cst[:, 64 * n:64 * n + 64], 77.0 * (n // 2) + 341.0 * (n % 2) + (488.0 if n > 1 else 0.0), "", "cst%d" % n)
    t1(T.pi[:, 0:1], T.i1[:, 0:1], -128.0, A.add, "i1", "pi0")
    cp(pf[7], T.i1[:, 0:1], "i1", "pf7")
    ts(T.li[:], T.i1[:], -1.0, pf[7], A.mult, A.add, "i1 pf7", "li", 128)
    t1(T.j2[:], T.li[:], 4, A.arith_shift_right, "li", "j2", 128)
    t1(T.pi[:, 1:2], T.pi[:, 0:1], 4, A.arith_shift_right, "pi0", "pi1")
    t1(T.pi[:, 2:3], T.pi[:, 0:1], 15, A.bitwise_and, "pi0", "pi2")
    t1(T.i1m[:], T.i1[:], 15, A.bitwise_and, "i1", "i1m", 128)
    t1(T.idn[:], T.i1[:], 128.0, A.is_equal, "i1", "idn", 128)
    cp(T.pf[:, 0:3], T.pi[:, 0:3], "pi0 pi1 pi2", "pf")
    t1(T.am[:], T.i1m[:], 0.0, A.is_equal, "i1m", "am", 128)
    t1(T.mr[:], T.li[:, 0:8], pf[1], A.is_equal, "li pf", "mr")
    t1(pf[4], pf[1], 128.0, A.mult, "pf", "pf4")
    t1(pf[9], pf[1], 4.0, A.mult, "pf", "pf9")
    ts(pf[6], pf[2], -100.0, pf[9], A.mult, A.add, "pf pf9", "pf6")
    t1(T.g8[0:8, :], T.j2[0:8, :], T.pf[0:8, 0:1], A.is_equal, "j2 pf", "g8", 128)
    for r in range(8):
        act(T.sel[:, 128 * r:128 * r + 128], T.am[:], "am mr", "sel%d" % r, 128, T.mr[:, r:r + 1])
    fn(T.mneg[:], T.am[:], AF.Identity, pf[13], 4096.0, "am pf13", "mneg", 128)
    t1(T.yi[:], T.b0[:], pf[4], A.add, "b0 pf4", "yi", 128)
    tt(T.yc[:], T.yi[:], T.mneg[:], A.add, "yi mneg", "yc", 256)
    t1(T.lanec[:], T.ln[:], pf[4], A.add, "ln pf4", "lanec", 128)
    t1(T.blk[:], T.j2[:], pf[1], A.is_equal, "j2 pf", "blk", 128)
    act(T.b61[:], T.blk[:], "blk", "b61", 128, 30.5)
    for name, c in (("idq", 2.0 ** -13), ("ndq", -2.0 ** -13), ("nid", -1.0), ("idh", 0.5), ("id9", 2.0 ** -9)):
        act(T[name][:], T.idn[:], "idn", name, 128, c)
    for t in range(4):
        ts(T.lr[:, 32 * t:32 * t + 32], T.li[:, 0:32], -1.0 * t, pf[6], A.add, A.is_equal, "li pf6", "lr%d" % t)
    sels, ys = names("sel", 8), [T.pb[:, 0:64], T.pb[:, 64:128]]

    def repeat(tag, b, src, name, start, stop):
        mmul(tag, b, [(T[b][:, 64 * r:64 * r + 64], T.sel[:, 128 * r:128 * r + 128], src, name + sels) for r in range(8)], start, stop)

    def places(t, h):
        return [(ys[p], T.idn[:], x, "idn yc cst%d" % (2 * t + p)) for p in range(2)
                for x in (T.yc[:, half(h)], T.cst[:, half(2 * t + p)])]

    def lists(h):
        s, l = str(h), half(h, 0, 8)
        op("v", lambda: V.tensor_tensor_scan(T.sc[:], T.keep[:], T.pb[:, 0:128], 0.0, A.mult, A.max), "keep pb", "sc", cost(128),
           tag="sc" + s)
        t1(T.oj[:, l], T.sc[:, 15:128:16], 1023, A.bitwise_and, "sc", "oj" + s)
        cp(T.o16[:, l], T.oj[:, l], "oj" + s, "o16" + s)

    for h in both:
        mmul("y", "pb", places(0, h))
        lists(h)

    now[0] = -1
    for h in both:
        s, b = str(h), ("pb", "pa")[h]
        t1(T.x16[:, half(h)], T.cc[:, h:128:2], -2048.0, A.add, "cc", "x16" + s)
        repeat("vt" + s, b, T.x16[:, half(h)], "x16" + s, "each", True)
        act(T.vt[:, h:1024:2], T[b][:], b, "vt%d@0" % h, 512)
    cp(T.memf[0:8, 0:128], T.memr[0:8, :], "memr", "memf", 128)
    mmul("mem", "pc0", [(T.pc0[:, half(h)], T.g8[0:8, :], T.memf[0:8, h:128:2], "g8 memf") for h in both], "each")
    ts(T.tq[:], T.pc0[:, 0:128], pf[2], -8192.0, A.not_equal, A.mult, "pc0 pf", "tq", 128)
    mmul("e", "pc1", [(T.pc1[:, 0:128], T.idn[:], T.lanec[:], "idn lanec"), (T.pc1[:, 0:128], T.idn[:], T.tq[:], "tq")], n=128)
    tt(T.xs[:], T.x16[:], T.pc1[:, 0:128], A.max, "pc1 x160 x161", "xs0 xs1", 128)
    t1(T.om16[:], T.oo[:], -2048.0, A.add, "oo", "om16", 128)
    ts(T.pe0[:, 0:128], T.oo[:], -6048.0, 4000.0, A.mult, A.add, "oo", "pe0", 128)
    tt(T.low0[:], T.om16[:], T.pe0[:, 0:128], A.max, "om16 pe0", "low0", 128)
    for h in both:
        b = "pk%d" % h
        repeat("kt%d" % h, b, T.low0[:, h:128:2], "low0", "each", True)
        cp(T.kt[:, h:1024:2], T[b][:], b, "kt%d@0" % h, 512)
    for h in both:
        fn(T["pc%d" % h][:, 320:384], T.pc1[:, half(h)], AF.Relu, pf[10], 1.0, "pc1 pf10", "pc%d" % h, tag="e%d" % h)
    fn(T.onep[:], T.tq[:], AF.Relu, pf[11], 0.125, "tq pf11", "onep", 128)
    cp(T.memf[0:8, 128:136], T.th8[0:8, :], "th8", "thf")
    mmul("th", "pa", [(T.pa[:, 0:8], T.g8[0:8, :], T.memf[0:8, 128:136], "g8 thf")])
    thc = [T.thc[:, k:k + 1] for k in range(3)]
    for k, (scale, bias) in enumerate(((-1.0, 0.5), (-1.0, 2.5), (2.0, -16.0))):
        ts(thc[k], T.pa[:, me:me + 1], scale, bias, A.mult, A.add, "pa", "thc%d" % k)
    mmul("zb", "pa", [(T.pa[:, 0:128], T.idn[:], T.tq[:], "idn tq"), (T.pa[:, 0:128], T.nid[:], T.lanec[:], "nid lanec")], n=128)
    t1(T.zb[:], T.pa[:, 0:128], -4000.0, A.max, "pa", "zb", 128)
    for h in both:
        b = "pc%d" % h
        mmul("one%d" % h, b, [(T[b][:, 256:320], T.idn[:], T.onep[:, half(h)], "idn onep")])

    def front(t, h, vts):
        s, c, B, last = str(h), half(h), 1024 * (t + 1), t == 3
        new = " o16%s vt0@%d vt1@%d" % (s, t, t)
        xn = ("xf" if last else "x16") + s
        x, win, at = T[xn[:-1]][:, c], T.vt[:, B - 1024:B], 1024 * h
        tt(T.x1[:, c], win.indirect(T.o16[:, 8 * h:8 * h + 4]), T.xs[:, c], A.max, "xs" + s + new, "x1" + s, 120)
        tt(x, win.indirect(T.o16[:, 8 * h + 4:8 * h + 8]), T.x1[:, c], A.max, "x1" + s + new, xn, 120)
        ts(T.off[:, c], x, B - 2048.0, 2048.0, A.min, A.add, xn, "off" + s)
        for n, (lo, hi) in enumerate(PIECES):
            act(T.gb[:, at + 16 * lo:at + 16 * hi], T.vt[:, 0:B + 1].indirect(T.off[:, 64 * h + lo:64 * h + hi]),
                "off" + s + vts, "g%s%s" % ("ab"[n], s), 15 + 25 * (hi - lo))
        if last:
            t1(T.xo[:, h:128:2], x, 2048.0, A.add, xn, "xo" + s)
            return
        repeat("vt" + s, "pa", x, xn, "each", True)
        act(T.vt[:, B + h:B + 1024:2], T.pa[:], "pa", "vt%d@%d" % (h, t + 1) + (vts if h == 0 else ""), 512)

    def keys(t, h):
        s, c = str(h), half(h)
        pe, pk, low = "pe" + s, "pk" + s, T.low[:, c]
        t8, tn = T.t8[:, half(h, 128 * t)], "t8%d@%d" % (h, t)
        win, kn = T.kt[:, half(t % 2, 0, 1024)], " o16%s kt0@%d kt1@%d" % (s, t % 2, t % 2)
        one, two = win.indirect(T.o16[:, 8 * h:8 * h + 4]), win.indirect(T.o16[:, 8 * h + 4:8 * h + 8])
        if t == 0:
            tt(T.k1[:, c], one, T.low0[:, h:128:2], A.min, "low0" + kn, "k1" + s, 120)
            tt(low, two, T.k1[:, c], A.min, "k1" + s + kn, "k2%s low%s" % (s, s), 120)
        else:
            tt(T.k1[:, c], one, T.ownk[:, c], A.max, "ownk" + s + kn, "k1" + s, 120)
            tt(T.k2[:, c], two, T.k1[:, c], A.max, "k1" + s + kn, "k2" + s, 120)
            ts(t8, T.k2[:, c], MAGIC, -MAGIC, A.add, A.add, "k2" + s, tn)
            tt(low, t8, T.k2[:, c], A.subtract, tn + " k2" + s, "low" + s, 128)
        mmul("low" + s, pe, [(T[pe][:, k:256:4], T.idn[:], low, "idn low" + s) for k in range(4)], "each")
        if t == 3:
            ts(T.t2[:, c], low, 3500.0, -6048.0, A.is_ge, A.mult, "low" + s, "t2" + s)
            mmul("mark" + s, pk, [(T[pk][:, 0:64], T.idn[:], x, "idn c2k low%s t2%s" % (s, s)) for x in (T.c2k[:, c], low, T.t2[:, c])],
                 True, False)
            return
        if t > 0:
            repeat("kT" + s, pk, t8, tn, True, False)

    def back(t, h):
        s, c, last = str(h), half(h), t == 3
        xn = "xf" if last else "x16"
        t8, tn = T.t8[:, half(h, 128 * t)], "t8%d@%d" % (h, t)
        up, un = T.up[:, half(h, 128 * t)], "up%d@%d" % (h, t)
        pe, pk, pc, at = "pe" + s, "pk" + s, "pc" + s, 1024 * h
        low, cnt, gbs, b = T[pe][:, 0:256:4], T[pc][:, 0:64], " ga%s gb%s" % (s, s), ("pb", "pa")[h]
        for k in range(4):
            f, m, name = at + 256 * k, "idn", "f%s%s" % ("abcd"[k], s)
            if k == 2:
                tt(T.sf[:, c], T[xn][:, c], low, A.is_ge, xn + s + " " + pe, "sf" + s)
                mmul("sf" + s, pc, [(cnt, T.idn[:], T.sf[:, c], "idn sf" + s)], False, False)
            if last and k == 1:
                m = "idh"
                mmul("g" + s, b, [(T[b][:, 256:512], T.idn[:], T.gb[:, at + k:at + 1024:4], "idn" + gbs)], True, False, 256)
                mmul("gl" + s, b, [(T[b][:, 256 + n:512:4], T.nid[:], T.low[:, c], "nid low" + s) for n in range(4)], False, True)
                fn(T.f1[:, f:f + 256], T[b][:, 256:512], AF.Sign, pf[12], 1.0, b + " pf12", name, 256)
            else:
                tt(T.f1[:, f:f + 256], T.gb[:, at + k:at + 1024:4], T[pe][:, 0:256], A.is_ge, pe + gbs, name, 256)
            mmul(name, pc, [(cnt, T[m][:], T.f1[:, f + n:f + 256:4], m + " " + name) for n in range(4)], k == 0, k == 3)
        if not last:
            d = T[pe][:, 320:384]
            mmul("d" + s, pe, [(d, T.idq[:], T.zb[:, c], "idq zb")] + [(d, T.ndq[:], T.onep[:, c], "ndq onep")] * t +
                 [(d, T.idq[:], T.low[:, c], "low" + s)])
        fn(T.ft[:, c], cnt, AF.Sign, thc[1 if last else 0], 1.0, pc + " thc0 thc1", "ft" + s)
        mmul("S" + s, pc, [(T[pc][:, 64:128], T.blk[:], T.ft[:, c], "blk ft" + s)])
        if not last:
            mmul("y" + s, "pb", places(t + 1, h) + [(y, T.id9[:], t8, "id9 " + tn) for y in ys if t > 0], True, False)
            mmul("yS" + s, "pb", [(y, T.b61[:], T.ft[:, c], "b61 ft" + s) for y in ys], False, False)
        ts(up, T[pc][:, 64:128], thc[2], 8192.0, A.is_ge, A.mult, pc + " thc2", un)
        if last:
            mmul("mup" + s, pk, [(T[pk][:, 0:64], T.nid[:], up, "nid " + un)], False, True)
            tt(T.mm[:, c], T[pc][:, 320:384], up, A.min, pc + " " + un, "mm" + s)
            tt(T.wo[:, h:128:2], T.mm[:, c], T[pk][:, 0:64], A.max, "mm%s %s" % (s, pk), "wo" + s)
            r = T[b][0:32, 0:64]
            terms = [(r, T.lr[:, 32 * u:32 * u + 32], T[src][:, half(h, 128 * u)], "lr%d %s%d@%d" % (u, src, h, u))
                     for u, src in ((0, "up"), (1, "t8"), (1, "up"), (2, "t8"), (2, "up"), (3, "t8"), (3, "up"))]
            mmul("R" + s, b, terms[:6], True, False)
            mmul("Rup" + s, b, terms[6:], False, True)
            act(T.rc[0:32, h:128:2], r, b, "rc" + s, scale=2.0 ** -13)
            return
        mmul("yup" + s, "pb", [(y, T.id9[:], up, "id9 " + un) for y in ys], False, True)
        tt(T.mm[:, c], T[pe][:, 320:384], up, A.mult, pe + " " + un, "mm" + s)
        tt(T.z16[:, c], T.mm[:, c], low, A.subtract, "mm%s %s" % (s, pe), "z16" + s)
        repeat("kup" + s, pk, up, un, t == 0, False)
        repeat("kz" + s, pk, T.z16[:, c], "z16" + s, False, True)
        n = (t + 1) % 2
        act(T.kt[:, 1024 * n + h:1024 * n + 1024:2], T[pk][:], pk, "kt%d@%d" % (h, n), 512)
        o = T[pc][:, 128:192]
        mmul("own" + s, pc, [(o, T.idn[:], up, "idn " + un)] + [(o, T.idn[:], t8, tn)] * (t > 0))
        tt(T.ownk[:, c], T.z16[:, c], o, A.add, pc + " z16" + s, "ownk" + s)
        tt(T.xs[:, c], T.x16[:, c], T[pc][:, 256:320], A.add, pc + " x16" + s, "xs" + s)
        lists(h)

    vts = " vt"
    for t in range(4):
        now[0] = t
        vts += " vt0@%d vt1@%d" % (t, t)
        for h in both:
            front(t, h, vts)
        if t == 3:
            dma("s", T.stgx[:], T.xo[:], "xo0 xo1", "stgx", "putx")
            dma("s", T.lndx[me], T.xo[mine, :], "xo0 xo1", "ownx", "ownx")
            exchange("x")
        for h in both:
            keys(t, h)
        for h in both:
            back(t, h)

    dma("s", T.stgw[:], T.wo[:], "wo0 wo1", "stgw", "putw")
    dma("a", T.stgr[:], T.rc[0:32, :], "rc0 rc1", "stgr", "putr")
    dma("s", T.lndw[me], T.wo[mine, :], "wo0 wo1", "ownw", "ownw")
    dma("a", T.lndr[me], T.rc[4 * me:4 * me + 4, :], "rc0 rc1", "ownr", "ownr")
    dma("s", T.yx[:], T.lndx[:], "lndx ownx", "yx", "ldx")
    exchange("r")
    exchange("w")
    dma("s", T.yo[:], T.lndw[:], "lndw ownw", "yo", "ldw")
    dma("a", T.yr[:], T.lndr[:], "lndr ownr", "yr", "ldr")
    emit(ops, g, T, arrivals)
